import numpy as np
import ml_dtypes


def mxq(x, axis, fmt="e4m3"):
    dtype, down = {"e4m3": (ml_dtypes.float8_e4m3fn, 7), "e5m2": (ml_dtypes.float8_e5m2, 14)}[fmt]
    v = np.moveaxis(np.asarray(x, np.float32).astype(ml_dtypes.bfloat16).astype(np.float64), axis, -1)
    blocks = v.reshape(v.shape[:-1] + (-1, 32))
    amax = np.abs(blocks).max(-1, keepdims=True)
    byte = np.maximum(np.where(amax > 0, np.frexp(amax)[1] - 1 + 127, 0) - down, 1)
    scale = np.exp2(byte - 127.0)
    codes = (blocks / scale).astype(np.float32).astype(dtype).astype(np.float64)
    return np.moveaxis((codes * scale).reshape(v.shape), -1, axis)


WIDE = False


def mx_kscale(k):
    if not WIDE:
        return np.ones(k)
    levels = np.array([10, -10, 5, -5, 0])
    if k % 512:
        return np.exp2(np.random.permutation(np.resize(levels, k // 32))).repeat(32)
    a = np.empty((k // 512, 16))
    for p in range(k // 512):
        a[p, :8] = np.random.permutation(np.resize(levels, 8))
        for g in range(8):
            far = levels[np.abs(levels - a[p, g]) >= 10]
            a[p, g + 8] = far[np.random.randint(len(far))]
    return np.exp2(a.ravel()).repeat(32)


BF16 = ml_dtypes.bfloat16


def bf(x):
    return np.asarray(x, np.float32).astype(BF16)


def f64(x):
    return np.asarray(x).astype(np.float64)


E2M1 = np.array([0.0, 0.5, 1.0, 1.5, 2.0, 3.0, 4.0, 6.0, -0.0, -0.5, -1.0, -1.5, -2.0, -3.0, -4.0, -6.0])


def pack_weight(w, fmt):
    k, n = w.shape
    w = f64(bf(w)).reshape(k // 32, 32, n)
    amax = np.abs(w).max(1)
    if fmt == "e4m3":
        byte = np.frexp(amax)[1] - 1 + 127 - 7
    else:
        mant, ex = np.frexp(amax / 6.0)
        byte = np.where(mant > 0.5, ex, ex - 1) + 127
    byte = np.clip(np.where(amax > 0, byte, 1), 1, 254)
    scaled = (w * np.exp2(127.0 - byte)[:, None, :]).reshape(k, n).astype(np.float32)
    by_word = np.ascontiguousarray(scaled.reshape(k // 512, 128, 4, n).transpose(0, 1, 3, 2))
    if fmt == "e4m3":
        words = by_word.astype(ml_dtypes.float8_e4m3fn).view(np.uint8)
    else:
        c = by_word.astype(ml_dtypes.float4_e2m1fn).view(np.uint8) & 0xF
        words = c[..., 0::2] | (c[..., 1::2] << 4)
    return np.ascontiguousarray(words), np.ascontiguousarray(byte.astype(np.uint8).reshape(k // 512, 16, n))


def unpack_weight(words, scales, fmt):
    g, p, n, _ = words.shape
    if fmt == "e4m3":
        vals = np.ascontiguousarray(words).view(ml_dtypes.float8_e4m3fn).astype(np.float64)
    else:
        nib = np.empty((g, p, n, 4), np.uint8)
        nib[..., 0::2] = words & 0xF
        nib[..., 1::2] = words >> 4
        vals = E2M1[nib]
    vals = vals * np.repeat(np.exp2(scales.astype(np.float64) - 127.0), 8, axis=1)[..., None]
    return vals.transpose(0, 1, 3, 2).reshape(g * 512, n)
def pack4(w):
    words, scales = pack_weight(w, "e2m1")
    return words.reshape(words.shape[0], 128, -1), scales


def unpack4(words, scales):
    return unpack_weight(words.reshape(words.shape[0], 128, -1, 2), scales, "e2m1")


def planes(Y):
    n, m = Y.shape
    b = f64(bf(Y)).reshape(n // 32, 32, m)
    amax = np.abs(b).max(1)
    byte = np.clip(np.where(amax > 0, np.frexp(amax)[1] - 1 + 127 - 7, 1), 1, 254)
    codes = (b * np.exp2(127.0 - byte)[:, None, :]).reshape(n, m).astype(np.float32).astype(ml_dtypes.float8_e4m3fn).view(np.uint8)
    words = codes.reshape(n // 512, 128, 4, m).transpose(0, 1, 3, 2)
    return np.ascontiguousarray(words), np.ascontiguousarray(byte.astype(np.uint8).reshape(n // 512, 16, m))


T, K, F, D = 768, 2048, 1536, 2048

def setup_inputs():
    s = mx_kscale(K)
    t = mx_kscale(F)
    x = np.random.randn(K, T) * s[:, None]
    adapter = np.random.randn(K, F) / np.sqrt(K) / s[:, None] * t[None, :]
    x_words, x_scales = pack_weight(x, "e4m3")
    adapter_words, adapter_scales = pack4(adapter)
    return {
        "x_words": x_words,
        "x_scales": x_scales,
        "adapter_words": adapter_words,
        "adapter_scales": adapter_scales,
        "adapter_bias": bf(0.3 * np.random.randn(F) * t),
        "proj": bf(np.random.randn(F, D) * np.sqrt(2.0 / F) / t[:, None]),
        "proj_bias": bf(0.3 * np.random.randn(D)),
        "feature_gain": bf(np.exp(0.8 * np.random.randn(D))),
        "time_embed": bf(0.3 * np.random.randn(T, D)),
    }

def reference(x_words, x_scales, adapter_words, adapter_scales, adapter_bias, proj, proj_bias, feature_gain, time_embed):
    X = unpack_weight(x_words, x_scales, "e4m3")
    A = unpack4(adapter_words, adapter_scales)
    h = np.maximum((X.T @ A) + f64(adapter_bias), 0.0)
    z = mxq(h, 1, "e4m3") @ mxq(f64(proj), 0, "e4m3")
    y = (z + f64(proj_bias)) * f64(feature_gain) + f64(time_embed)
    Y = y.T
    words, scales = planes(Y)
    return y, words, scales

@@ -1,0 +1,397 @@
+from contextlib import ExitStack
+
+import concourse.mybir as mybir
+from concourse.masks import make_identity
+
+T, K, F, D = 768, 2048, 1536, 2048
+FLOPS = 2 * T * K * F + 2 * T * F * D
+
+F32 = mybir.dt.float32
+BF16 = mybir.dt.bfloat16
+I32 = mybir.dt.int32
+U32 = mybir.dt.uint32
+U8 = mybir.dt.uint8
+FP8X4 = mybir.dt.float8_e4m3fn_x4
+FP4X4 = mybir.dt.float4_e2m1fn_x4
+ACT = mybir.ActivationFunctionType
+ALU = mybir.AluOpType
+
+P = 128
+KP = K // 512
+FP = F // 512
+SLOTS = 4 * FP
+CHUNKS = D // 512
+GROUPS = ((0, 512), (512, 256))
+BANKS = 8
+EARLY = 4
+CAST = "vvvvvvvvsvvv"
+FILL = {
+    (0, 0): [("aw", 1, 0), ("as", 1, 0)],
+    (1, 0): [("as", 2, 0), ("pv", 0, 0)],
+    (1, 2): [("aw", 2, 0), ("ps0", 1, 0), ("ps1", 1, 0), ("pq", 0, 0)],
+    (1, 4): [("pq", 1, 0)],
+    (1, 5): [("hi", 0, 0)],
+    (1, 7): [("pv", 0, 1), ("hi", 0, 1)],
+    (1, 8): [("pq", 0, 1)],
+    (1, 9): [("hq", 0, 0)],
+    (1, 10): [("hq", 0, 1)],
+    (1, 12): [("ps0", 1, 2)],
+    (1, 13): [("hi", 0, 2), ("ps1", 1, 2), ("pv", 1, 1), ("pq", 1, 2), ("hq", 0, 2), ("ps0", 2, 0)],
+    (1, 14): [("pv", 0, 2)],
+    (1, 15): [("hi", 1, 0)],
+    (1, 17): [("ps1", 2, 0), ("pq", 0, 2)],
+    (1, 19): [("pq", 2, 0)],
+    (1, 21): [("pq", 1, 1)],
+    (1, 22): [("hq", 1, 0)],
+    (2, 0, 0, 2): [("hi", 1, 1), ("hi", 1, 2)],
+    (2, 0, 0, 3): [("hq", 1, 1), ("hq", 1, 2)],
+    (2, 1, 0, 0): [("pv", 3, 0)],
+    (2, 1, 0, 1): [("ps0", 2, 2)],
+    (2, 0, 1, 0): [("pv", 2, 1)],
+    (2, 0, 1, 1): [("ps1", 2, 2)],
+    (2, 0, 1, 2): [("pq", 2, 2)],
+    (2, 2, 0, 2): [("pq", 2, 1)],
+    (2, 1, 1, 1): [("pq", 3, 0)],
+    (2, 3, 0, 0): [("ps0", 3, 1)],
+    (2, 2, 1, 0): [("pv", 3, 2), ("ps1", 3, 1)],
+    (2, 4, 0, 1): [("pq", 3, 2)],
+    (2, 5, 0, 1): [("pq", 3, 1)],
+}
+TAIL = ((0, 256), (256, 256), (512, 128), (640, 128))
+
+
+def tile_speech_adapter_to_language_h2_kernel(
+    tc, x_words, x_scales, adapter_words, adapter_scales, adapter_bias, proj, proj_bias,
+    feature_gain, time_embed, out_0, out_1, out_2,
+):
+    nc = tc.nc
+    with ExitStack() as ctx:
+        keep = ctx.enter_context(tc.tile_pool(name="keep", bufs=1))
+        work = ctx.enter_context(tc.tile_pool(name="work", bufs=2))
+        psum = ctx.enter_context(tc.psum_pool(name="psum", bufs=1))
+        ctx.enter_context(tc.manual_schedule())
+
+        def bank(n):
+            return psum.tile([P, 512], F32, name="bank%d" % n, tag="bank%d" % n)
+
+        xw = [keep.tile([P, KP, n], U32, name="xw%d" % t0, align_bytes=64) for (t0, n) in GROUPS]
+        xs = keep.tile([P, KP, T], U8, name="xs", align_bytes=64)
+        aw = keep.tile([P, FP, KP, 1024], U8, name="aw", align_bytes=64)
+        asc = keep.tile([P, FP, KP, 512], U8, name="asc", align_bytes=64)
+        aw_raw = [
+            work.tile([P, KP, 256], I32, name="aw_raw%d" % h, tag=("yb", "yb", "yi")[h], bufs=2, align_bytes=64)
+            for h in range(FP)
+        ]
+        as_first = work.tile([P, KP, 128], I32, name="as_first", tag="zg", bufs=2, align_bytes=64)
+        as_rest = work.tile([P, KP, 256], I32, name="as_rest", tag="zg", bufs=2, align_bytes=64)
+        pw = keep.tile([P, FP, D], U32, name="pw", align_bytes=64)
+        ps = keep.tile([P, FP, D], U8, name="ps", align_bytes=64)
+        hw = keep.tile([P, FP, T], U32, name="hw", align_bytes=64)
+        hs = keep.tile([P, FP, T], U8, name="hs", align_bytes=64)
+        ysc = keep.tile([P, CHUNKS, T], U8, name="ysc", align_bytes=64)
+        vec = keep.tile([P, FP * P], BF16, name="vec")
+        vec32 = keep.tile([P, FP * P], F32, name="vec32")
+        ident = keep.tile([P, P], F32, name="ident")
+        consts = keep.tile([P, FP * P], F32, name="consts")
+        bias_gain = keep.tile([P, 16], F32, name="bias_gain")
+        warm = keep.tile([P, 8], F32, name="warm")
+
+        x_codes = x_words.rearrange("g p n t -> p g (n t)").bitcast(I32)
+        a_codes = adapter_words.rearrange("g p n -> p g n").bitcast(I32)
+
+        a_scales = adapter_scales.rearrange("g q n -> q g n").bitcast(I32)
+        x_rows = x_scales.rearrange("g q n -> q g n").bitcast(I32)
+        proj_rows = proj.rearrange("(h b t r) d -> h r b t d", h=FP, t=4, r=8)
+        praw = {}
+        te = {}
+
+        def load_adapter(h, g0, g1):
+            nc.sync.dma_start(out=aw_raw[h][:, g0:g1, :], in_=a_codes[:, g0:g1, 256 * h : 256 * (h + 1)])
+
+        def load_frames(g0, g1):
+            nc.sync.dma_start(out=xw[0][:, g0:g1, :].bitcast(I32), in_=x_codes[:, g0:g1, 0:512])
+
+        def load_scale_rows(queue, plane, rows, q):
+            queue.dma_start(out=plane[32 * q : 32 * q + 4, :, :], in_=rows[4 * q : 4 * q + 4, :, :])
+
+        def load_proj(half, h):
+            praw[half, h] = work.tile([P, 4, 1024], BF16, name="praw%d%d" % (half, h), tag="praw", bufs=2 * FP)
+            for r in (0, 4, 1, 5, 2, 6, 3, 7):
+                nc.sync.dma_start(
+                    out=praw[half, h][r:P:8, :, :], in_=proj_rows[h][r][:, :, 1024 * half : 1024 * (half + 1)]
+                )
+
+        def load_te(c):
+            if c < 2:
+                te[c] = keep.tile([P, T // P, 512], BF16, name="te%d" % c)
+            else:
+                te[c] = work.tile([P, T // P, 512], BF16, name="te%d" % c, tag="praw", bufs=2 * FP)
+            nc.sync.dma_start(
+                out=te[c][:], in_=time_embed[:, 512 * c : 512 * (c + 1)].rearrange("(j p) d -> p j d", p=P)
+            )
+
+        def permute_words(h, g0, g1):
+            nc.vector.tensor_copy(
+                out=aw[:, h, g0:g1, :].bitcast(I32).rearrange("p g (t b w) -> p g t b w", t=4, w=4),
+                in_=aw_raw[h][:, g0:g1, :].rearrange("p g (b t w) -> p g t b w", t=4, w=4),
+            )
+
+        def permute_scales(h):
+            rows = as_first[:] if h == 0 else as_rest[:, :, 128 * (h - 1) : 128 * h]
+            nc.vector.tensor_copy(
+                out=asc[:, h, :, :].bitcast(I32).rearrange("p g (t b w) -> p g t b w", t=4, w=2),
+                in_=rows.rearrange("p g (b t w) -> p g t b w", t=4, w=2),
+            )
+
+        nc.vector.memset(as_first[:], 0)
+        nc.gpsimd.memset(xs[:].bitcast(I32), 0)
+        nc.vector.memset(as_rest[:], 0)
+        nc.vector.memset(vec[:], 0.0)
+        nc.vector.memset(warm[:], 0.0)
+        nc.scalar.activation(out=warm[:, 0:1], in_=warm[:, 4:5], func=ACT.Relu)
+        load_adapter(0, 0, 1)
+        load_frames(0, 1)
+        for q in range(4):
+            load_scale_rows(nc.sync, as_first, a_scales[:, :, 0:128], q)
+        for q in range(4):
+            load_scale_rows(nc.sync if q % 2 == 0 else nc.gpsimd, xs[:].bitcast(I32), x_rows, q)
+        nc.gpsimd.dma_start(
+            out=vec[0:4, :].rearrange("t (n r) -> t n r", r=8),
+            in_=adapter_bias.rearrange("(n t r) -> t n r", t=4, r=8),
+        )
+        nc.gpsimd.dma_start(out=vec[32:48, 0:P], in_=proj_bias.rearrange("(i p) -> i p", p=P))
+        nc.gpsimd.dma_start(out=vec[64:80, 0:P], in_=feature_gain.rearrange("(i p) -> i p", p=P))
+        make_identity(nc, ident[:])
+        load_adapter(0, 1, KP)
+        load_frames(1, 2)
+        load_frames(2, KP)
+        load_adapter(1, 0, KP)
+        for q in range(4):
+            load_scale_rows(nc.sync, as_rest, a_scales[:, :, 128:384], q)
+        load_proj(0, 0)
+        load_adapter(2, 0, KP)
+        load_proj(0, 1)
+        nc.sync.dma_start(out=xw[1][:].bitcast(I32), in_=x_codes[:, :, 512:T])
+        load_proj(0, 2)
+        load_proj(1, 0)
+        load_te(0)
+        load_proj(1, 1)
+        load_te(1)
+        load_proj(1, 2)
+
+        permute_words(0, 0, 1)
+        permute_scales(0)
+        permute_words(0, 1, KP)
+        nc.vector.tensor_copy(out=vec32[:], in_=vec[:])
+
+        def adapter_pass(acc, s, g, t0, n, col):
+            nc.tensor.matmul_mx(
+                out=acc[:, col : col + n],
+                lhsT=aw[:, s // 4, g, 256 * (s % 4) : 256 * (s % 4 + 1)].bitcast(FP4X4),
+                lhsT_scale=asc[:, s // 4, g, P * (s % 4) : P * (s % 4 + 1)],
+                rhs=xw[t0 // 512][:, g, t0 % 512 : t0 % 512 + n].bitcast(FP8X4),
+                rhs_scale=xs[:, g, t0 : t0 + n],
+                start=(g == 0),
+                stop=(g == KP - 1),
+            )
+
+        hrelu = {}
+
+        def relu(acc, grp, s):
+            n = GROUPS[grp][1]
+            if s % 4 == 0:
+                hrelu[grp, s // 4] = work.tile([P, 4, n], BF16, name="hrelu", tag="hrelu", bufs=2)
+            nc.scalar.activation(
+                out=hrelu[grp, s // 4][:, s % 4, :], in_=acc[:, 0:n], func=ACT.Relu, bias=consts[:, P * (s // 4) + s % 4 : P * (s // 4) + s % 4 + 1]
+            )
+
+        inter = {}
+
+        def interleave(engine_copy, key, rows, c0, c1):
+            if c0 == 0:
+                inter[key] = work.tile([P, rows.shape[2], 4], BF16, name="inter", tag="inter", bufs=4, align_bytes=64)
+            engine_copy(
+                out=inter[key][:, c0:c1, :].rearrange("p (c i) t -> p c t i", i=4),
+                in_=rows[:, :, c0:c1].rearrange("p t (c i) -> p c t i", i=4),
+            )
+
+        def quantize(key, words, scales):
+            nc.vector.quantize_mx(
+                out=words.bitcast(FP8X4), scales=scales, in_=inter[key][:].rearrange("p n t -> p (n t)")
+            )
+
+        def job(kind, a, b):
+            if kind == "hi":
+                interleave(nc.vector.tensor_copy, ("h", a, b), hrelu[a, b], 0, GROUPS[a][1])
+            elif kind == "hq":
+                t0, n = GROUPS[a]
+                quantize(("h", a, b), hw[:, b, t0 : t0 + n], hs[:, b, t0 : t0 + n])
+            elif kind == "pv":
+                interleave(nc.vector.tensor_copy, ("p", a, b), praw[a // 2, b][:, :, 512 * (a % 2) : 512 * (a % 2 + 1)], 0, 512)
+            elif kind == "ps0":
+                interleave(nc.scalar.copy, ("p", a, b), praw[a // 2, b][:, :, 512 * (a % 2) : 512 * (a % 2 + 1)], 0, 256)
+            elif kind == "ps1":
+                interleave(nc.scalar.copy, ("p", a, b), praw[a // 2, b][:, :, 512 * (a % 2) : 512 * (a % 2 + 1)], 256, 512)
+            elif kind == "aw":
+                permute_words(a, 0, KP)
+            elif kind == "as":
+                permute_scales(a)
+            else:
+                cols = slice(512 * a, 512 * (a + 1))
+                quantize(("p", a, b), pw[:, b, cols], ps[:, b, cols])
+
+        def fill(*key):
+            for item in FILL.get(key, ()):
+                job(*item)
+
+        first = [bank(s) for s in range(EARLY)]
+        for g in range(KP - 1):
+            for s in range(EARLY):
+                adapter_pass(first[s], s, g, 0, 512, 0)
+        turned = bank(BANKS - 1)
+        for h in range(FP):
+            nc.tensor.transpose(turned[:, P * h : P * (h + 1)], vec32[:, P * h : P * (h + 1)], ident[:])
+        fill(0, 0)
+        nc.vector.tensor_copy(out=consts[:], in_=turned[:, 0 : FP * P])
+        nc.vector.tensor_tensor(out=bias_gain[:], in0=consts[:, 32:48], in1=consts[:, 64:80], op=ALU.mult)
+
+        for n in range(2 * SLOTS):
+            grp, s = divmod(n, SLOTS)
+            if n < EARLY:
+                acc = first[n]
+                adapter_pass(acc, s, KP - 1, 0, 512, 0)
+            elif grp == 0:
+                acc = bank(n % BANKS)
+                for g in range(KP):
+                    adapter_pass(acc, s, g, 0, 512, 0)
+            else:
+                acc = bank(n % BANKS)
+                for half in range(2):
+                    for g in range(KP):
+                        adapter_pass(acc, s, g, 512 + P * half, P, P * half)
+            relu(acc, grp, s)
+            fill(1, n)
+
+        units = [(c, t0, n) for c in range(CHUNKS) for (t0, n) in (GROUPS if c < CHUNKS - 1 else TAIL)]
+        zg, y, yb, yi = {}, {}, {}, {}
+        count = {"z": 0, "y": 0, "w": 0}
+
+        def next_bank(role, base, depth):
+            n = base + count[role] % depth
+            count[role] += 1
+            return bank(n)
+
+        def project(u):
+            c, t0, n = units[u]
+            zg[u] = work.tile([P, 4, n], F32, name="zg", tag="zg", bufs=2, align_bytes=64)
+            for i in range(4):
+                acc = next_bank("z", 0, 3)
+                cols = slice(512 * c + P * i, 512 * c + P * (i + 1))
+                for g in range(FP):
+                    nc.tensor.matmul_mx(
+                        out=acc[:, 0:n],
+                        lhsT=pw[:, g, cols].bitcast(FP8X4),
+                        lhsT_scale=ps[:, g, cols],
+                        rhs=hw[:, g, t0 : t0 + n].bitcast(FP8X4),
+                        rhs_scale=hs[:, g, t0 : t0 + n],
+                        start=(g == 0),
+                        stop=(g == FP - 1),
+                    )
+                m = 4 * c + i
+                nc.scalar.activation(
+                    out=zg[u][:, i, :], in_=acc[:, 0:n], func=ACT.Identity,
+                    scale=consts[:, 64 + m : 65 + m], bias=bias_gain[:, m : m + 1],
+                )
+                fill(2, u, 0, i)
+
+        def turn_back(u):
+            c, t0, n = units[u]
+            for j0 in range(0, n // P, 2):
+                nj = min(2, n // P - j0)
+                y[u, j0] = work.tile([P, nj, 512], F32, name="y", tag="y", bufs=6)
+                for j in range(j0, j0 + nj):
+                    acc = next_bank("y", 3, 4)
+                    for i in range(4):
+                        nc.tensor.transpose(acc[:, P * i : P * (i + 1)], zg[u][:, i, P * j : P * (j + 1)], ident[:])
+                    nc.vector.tensor_tensor(
+                        out=y[u, j0][:, j - j0, :], in0=acc[:], in1=te[c][:, t0 // P + j, :], op=ALU.add
+                    )
+                rows = slice(t0 + P * j0, t0 + P * (j0 + nj))
+                nc.sync.dma_start(
+                    out=out_0[rows, 512 * c : 512 * (c + 1)].rearrange("(j p) d -> p j d", p=P), in_=y[u, j0][:]
+                )
+
+        def round_rows(u, j0):
+            n = units[u][2]
+            j1 = min(j0 + 2, n // P)
+            if j0 == 0:
+                yb[u] = work.tile([P, n // P, 512], BF16, name="yb", tag="yb", bufs=2, align_bytes=64)
+            out = yb[u][:, j0:j1, :].rearrange("p j (v m e) -> p j v m e", v=2, e=2)
+            rows = y[u, j0][:].rearrange("p j (m v e) -> p j v m e", v=2, e=2)
+            if CAST[u] == "v":
+                nc.vector.tensor_copy(out=out, in_=rows)
+            elif CAST[u] == "s":
+                nc.scalar.copy(out=out, in_=rows)
+            else:
+                for j in range(j1 - j0):
+                    nc.gpsimd.tensor_scalar(out=out[:, j], in0=rows[:, j], scalar1=1.0, scalar2=0.0, op0=ALU.mult, op1=ALU.add)
+
+        def turn_words(u, j0):
+            n = units[u][2]
+            if j0 == 0:
+                yi[u] = work.tile([P, n, 4], BF16, name="yi", tag="yi", bufs=2, align_bytes=64)
+            pairs = yb[u][:].bitcast(F32)
+            acc = bank(BANKS - 1)
+            nj = min(2, n // P - j0)
+            for jj in range(nj):
+                for v in range(2):
+                    col = P * (2 * jj + v)
+                    nc.tensor.transpose(acc[:, col : col + P], pairs[:, j0 + jj, P * v : P * (v + 1)], ident[:])
+            nc.scalar.copy(
+                out=yi[u][:, P * j0 : P * (j0 + nj), :].bitcast(F32).rearrange("p (j m) v -> p j m v", j=nj),
+                in_=acc[:, 0 : 256 * nj].rearrange("p (j v m) -> p j m v", j=nj, v=2),
+            )
+
+        def planes(u):
+            c, t0, n = units[u]
+            yw = work.tile([P, n], U32, name="yw", tag="yw", bufs=3, align_bytes=64)
+            nc.vector.quantize_mx(
+                out=yw[:].bitcast(FP8X4), scales=ysc[:, c, t0 : t0 + n], in_=yi[u][:].rearrange("p n t -> p (n t)")
+            )
+            nc.sync.dma_start(
+                out=out_1[c].rearrange("p n t -> p (n t)").bitcast(I32)[:, t0 : t0 + n], in_=yw[:].bitcast(I32)
+            )
+
+        def store_scales(c0, c1):
+            for q in range(4):
+                nc.sync.dma_start(
+                    out=out_2[c0:c1, 4 * q : 4 * q + 4, :].rearrange("g r n -> r g n").bitcast(I32),
+                    in_=ysc[32 * q : 32 * q + 4, c0:c1, :].bitcast(I32),
+                )
+
+        last = len(units) - 1
+        load_te(2)
+        load_te(3)
+        project(0)
+        for u in range(last + 2):
+            if u < last:
+                project(u + 1)
+            wide = u >= 1 and units[u - 1][2] == 512
+            if wide:
+                turn_words(u - 1, 0)
+            fill(2, u, 1, 0)
+            if u <= last:
+                turn_back(u)
+            if u >= 1:
+                turn_words(u - 1, 2 if wide else 0)
+            fill(2, u, 1, 1)
+            if u <= last:
+                round_rows(u, 0)
+            if u >= 1:
+                planes(u - 1)
+            if u <= last and units[u][2] == 512:
+                round_rows(u, 2)
+            fill(2, u, 1, 2)
+            if u == 2 * CHUNKS - 2:
+                store_scales(0, CHUNKS - 1)
+        store_scales(CHUNKS - 1, CHUNKS)

@@ -23,39 +23,58 @@ SLOTS = 4 * FP
 CHUNKS = D // 512
 GROUPS = ((0, 512), (512, 256))
 BANKS = 8
-EARLY = 4
-CAST = "vvvvvvvvsvvv"
+EARLY = 8
+CAST = "v"
 FILL = {
-    (0, 0): [("aw", 1, 0), ("as", 1, 0)],
-    (1, 0): [("as", 2, 0), ("pv", 0, 0)],
-    (1, 2): [("aw", 2, 0), ("ps0", 1, 0), ("ps1", 1, 0), ("pq", 0, 0)],
-    (1, 4): [("pq", 1, 0)],
-    (1, 5): [("hi", 0, 0)],
-    (1, 7): [("pv", 0, 1), ("hi", 0, 1)],
-    (1, 8): [("pq", 0, 1)],
-    (1, 9): [("hq", 0, 0)],
-    (1, 10): [("hq", 0, 1)],
-    (1, 12): [("ps0", 1, 2)],
-    (1, 13): [("hi", 0, 2), ("ps1", 1, 2), ("pv", 1, 1), ("pq", 1, 2), ("hq", 0, 2), ("ps0", 2, 0)],
-    (1, 14): [("pv", 0, 2)],
-    (1, 15): [("hi", 1, 0)],
-    (1, 17): [("ps1", 2, 0), ("pq", 0, 2)],
-    (1, 19): [("pq", 2, 0)],
-    (1, 21): [("pq", 1, 1)],
-    (1, 22): [("hq", 1, 0)],
-    (2, 0, 0, 2): [("hi", 1, 1), ("hi", 1, 2)],
-    (2, 0, 0, 3): [("hq", 1, 1), ("hq", 1, 2)],
-    (2, 1, 0, 0): [("pv", 3, 0)],
-    (2, 1, 0, 1): [("ps0", 2, 2)],
-    (2, 0, 1, 0): [("pv", 2, 1)],
-    (2, 0, 1, 1): [("ps1", 2, 2)],
-    (2, 0, 1, 2): [("pq", 2, 2)],
-    (2, 2, 0, 2): [("pq", 2, 1)],
-    (2, 1, 1, 1): [("pq", 3, 0)],
-    (2, 3, 0, 0): [("ps0", 3, 1)],
-    (2, 2, 1, 0): [("pv", 3, 2), ("ps1", 3, 1)],
-    (2, 4, 0, 1): [("pq", 3, 2)],
-    (2, 5, 0, 1): [("pq", 3, 1)],
+    (0, 0): [("as", 2, 0), ("pv", 0, 0), ("as", 2, 2), ("ps0", 1, 0), ("ps1", 1, 0), ("as", 2, 1), ("aw", 2, 0)],
+    (1, 0): [("aw", 2, 2)],
+    (1, 1): [("aw", 2, 1), ("aw", 2, 3)],
+    (1, 2): [("pq", 1, 0)],
+    (1, 3): [("as", 2, 3)],
+    (1, 4): [("hi", 0, 0)],
+    (1, 6): [("pq", 0, 0)],
+    (1, 7): [("hq", 0, 0)],
+    (1, 9): [("hi", 0, 1), ("pv", 1, 2)],
+    (1, 10): [("pq", 1, 2), ("hq", 0, 1)],
+    (1, 11): [("ps0", 0, 1)],
+    (1, 12): [("ps1", 0, 1), ("hi", 0, 2)],
+    (1, 13): [("pv", 1, 1)],
+    (1, 15): [("pq", 0, 1), ("hq", 0, 2)],
+    (1, 19): [("hs", 1, 0), ("pv", 0, 2)],
+    (1, 22): [("pq", 1, 1), ("pq", 0, 2)],
+    (1, 23): [("hs", 1, 1), ("hi", 1, 2)],
+    (2, 0, 0, 0): [("hq", 1, 0)],
+    (2, 0, 0, 3): [("hq", 1, 2), ("hq", 1, 1), ("pv", 2, 2), ("pv", 2, 0)],
+    (2, 1, 0, 0): [("ps0", 3, 0)],
+    (2, 0, 1, 0): [("pv", 3, 1)],
+    (2, 0, 2, 0): [("pq", 2, 2)],
+    (2, 0, 2, 2): [("cv", 0, 0), ("ps1", 3, 0)],
+    (2, 2, 0, 0): [("pq", 2, 0)],
+    (2, 2, 0, 2): [("cv", 0, 2)],
+    (2, 1, 1, 0): [("pv", 2, 1)],
+    (2, 1, 2, 0): [("pq", 3, 1)],
+    (2, 3, 0, 1): [("cs", 1, 0)],
+    (2, 3, 0, 3): [("pq", 2, 1)],
+    (2, 2, 2, 2): [("yq", 0, 0)],
+    (2, 2, 1, 1): [("cs", 2, 0), ("yq", 1, 0), ("pv", 3, 2)],
+    (2, 4, 0, 1): [("cv", 2, 2)],
+    (2, 5, 0, 0): [("cs", 3, 0)],
+    (2, 5, 0, 1): [("pq", 3, 0)],
+    (2, 5, 0, 3): [("pq", 3, 2)],
+    (2, 4, 1, 0): [("yq", 2, 0)],
+    (2, 4, 2, 0): [("cv", 4, 0)],
+    (2, 6, 0, 3): [("cv", 4, 2)],
+    (2, 5, 2, 0): [("yq", 3, 0)],
+    (2, 5, 1, 1): [("yq", 4, 0)],
+    (2, 7, 0, 1): [("cv", 5, 0)],
+    (2, 8, 0, 0): [("yq", 5, 0)],
+    (2, 8, 0, 2): [("cv", 6, 0)],
+    (2, 9, 0, 1): [("cv", 7, 0)],
+    (2, 9, 0, 3): [("yq", 6, 0)],
+    (2, 9, 1, 0): [("cs", 8, 0)],
+    (2, 9, 1, 1): [("cv", 9, 0), ("yq", 7, 0)],
+    (2, 10, 1, 0): [("yq", 8, 0)],
+    (2, 10, 1, 1): [("yq", 9, 0)],
 }
 TAIL = ((0, 256), (256, 256), (512, 128), (640, 128))
 
@@ -78,21 +97,20 @@ def tile_speech_adapter_to_language_h2_kernel(
         xs = keep.tile([P, KP, T], U8, name="xs", align_bytes=64)
         aw = keep.tile([P, FP, KP, 1024], U8, name="aw", align_bytes=64)
         asc = keep.tile([P, FP, KP, 512], U8, name="asc", align_bytes=64)
-        aw_raw = [
-            work.tile([P, KP, 256], I32, name="aw_raw%d" % h, tag=("yb", "yb", "yi")[h], bufs=2, align_bytes=64)
-            for h in range(FP)
-        ]
-        as_first = work.tile([P, KP, 128], I32, name="as_first", tag="zg", bufs=2, align_bytes=64)
-        as_rest = work.tile([P, KP, 256], I32, name="as_rest", tag="zg", bufs=2, align_bytes=64)
+        aw_early = work.tile([P, KP, 2048], U8, name="aw_early", tag="zg", bufs=2, align_bytes=64)
+        aw_late = work.tile([P, KP, 1024], U8, name="aw_late", tag="yi", bufs=2, align_bytes=64)
+        as_first = work.tile([P, 1, F], U8, name="as_first", tag="yi", bufs=2, align_bytes=64)
+        as_rest = work.tile([P, KP - 1, F], U8, name="as_rest", tag="zg", bufs=2, align_bytes=64)
         pw = keep.tile([P, FP, D], U32, name="pw", align_bytes=64)
         ps = keep.tile([P, FP, D], U8, name="ps", align_bytes=64)
         hw = keep.tile([P, FP, T], U32, name="hw", align_bytes=64)
         hs = keep.tile([P, FP, T], U8, name="hs", align_bytes=64)
         ysc = keep.tile([P, CHUNKS, T], U8, name="ysc", align_bytes=64)
-        vec = keep.tile([P, FP * P], BF16, name="vec")
-        vec32 = keep.tile([P, FP * P], F32, name="vec32")
+        abias = keep.tile([P, FP, 4], BF16, name="abias")
+        vec = keep.tile([P, P], BF16, name="vec")
+        vec32 = keep.tile([P, P], F32, name="vec32")
         ident = keep.tile([P, P], F32, name="ident")
-        consts = keep.tile([P, FP * P], F32, name="consts")
+        consts = keep.tile([P, P], F32, name="consts")
         bias_gain = keep.tile([P, 16], F32, name="bias_gain")
         warm = keep.tile([P, 8], F32, name="warm")
 
@@ -101,25 +119,20 @@ def tile_speech_adapter_to_language_h2_kernel(
 
         a_scales = adapter_scales.rearrange("g q n -> q g n").bitcast(I32)
         x_rows = x_scales.rearrange("g q n -> q g n").bitcast(I32)
-        proj_rows = proj.rearrange("(h b t r) d -> h r b t d", h=FP, t=4, r=8)
+        proj_rows = proj.rearrange("(h p t) d -> h p t d", h=FP, t=4)
         praw = {}
         te = {}
 
-        def load_adapter(h, g0, g1):
-            nc.sync.dma_start(out=aw_raw[h][:, g0:g1, :], in_=a_codes[:, g0:g1, 256 * h : 256 * (h + 1)])
-
-        def load_frames(g0, g1):
-            nc.sync.dma_start(out=xw[0][:, g0:g1, :].bitcast(I32), in_=x_codes[:, g0:g1, 0:512])
+        def load_words(g):
+            nc.sync.dma_start(out=aw_early[:, g, :].bitcast(I32), in_=a_codes[:, g, 0:512])
+            nc.sync.dma_start(out=xw[0][:, g, :].bitcast(I32), in_=x_codes[:, g, 0:512])
 
         def load_scale_rows(queue, plane, rows, q):
-            queue.dma_start(out=plane[32 * q : 32 * q + 4, :, :], in_=rows[4 * q : 4 * q + 4, :, :])
+            queue.dma_start(out=plane[q:P:32, :, :], in_=rows[q:16:4, :, :])
 
         def load_proj(half, h):
             praw[half, h] = work.tile([P, 4, 1024], BF16, name="praw%d%d" % (half, h), tag="praw", bufs=2 * FP)
-            for r in (0, 4, 1, 5, 2, 6, 3, 7):
-                nc.sync.dma_start(
-                    out=praw[half, h][r:P:8, :, :], in_=proj_rows[h][r][:, :, 1024 * half : 1024 * (half + 1)]
-                )
+            nc.sync.dma_start(out=praw[half, h][:], in_=proj_rows[h][:, :, 1024 * half : 1024 * (half + 1)])
 
         def load_te(c):
             if c < 2:
@@ -130,46 +143,41 @@ def tile_speech_adapter_to_language_h2_kernel(
                 out=te[c][:], in_=time_embed[:, 512 * c : 512 * (c + 1)].rearrange("(j p) d -> p j d", p=P)
             )
 
-        def permute_words(h, g0, g1):
+        def permute_words(h, g):
+            rows = aw_early[:, g, 1024 * h : 1024 * (h + 1)] if h < 2 else aw_late[:, g, :]
             nc.vector.tensor_copy(
-                out=aw[:, h, g0:g1, :].bitcast(I32).rearrange("p g (t b w) -> p g t b w", t=4, w=4),
-                in_=aw_raw[h][:, g0:g1, :].rearrange("p g (b t w) -> p g t b w", t=4, w=4),
+                out=aw[:, h, g, :].rearrange("p (t m e) -> p t m e", t=4, e=2),
+                in_=rows.rearrange("p (m t e) -> p t m e", t=4, e=2),
             )
 
-        def permute_scales(h):
-            rows = as_first[:] if h == 0 else as_rest[:, :, 128 * (h - 1) : 128 * h]
+        def permute_scales(h, g):
+            rows = (as_first[:, 0, :] if g == 0 else as_rest[:, g - 1, :])[:, 512 * h : 512 * (h + 1)]
             nc.vector.tensor_copy(
-                out=asc[:, h, :, :].bitcast(I32).rearrange("p g (t b w) -> p g t b w", t=4, w=2),
-                in_=rows.rearrange("p g (b t w) -> p g t b w", t=4, w=2),
+                out=asc[:, h, g, :].rearrange("p (t m) -> p t m", t=4), in_=rows.rearrange("p (m t) -> p t m", t=4)
             )
 
-        nc.vector.memset(as_first[:], 0)
+        nc.vector.memset(as_first[:].bitcast(I32), 0)
         nc.gpsimd.memset(xs[:].bitcast(I32), 0)
-        nc.vector.memset(as_rest[:], 0)
+        nc.vector.memset(as_rest[:].bitcast(I32), 0)
         nc.vector.memset(vec[:], 0.0)
         nc.vector.memset(warm[:], 0.0)
         nc.scalar.activation(out=warm[:, 0:1], in_=warm[:, 4:5], func=ACT.Relu)
-        load_adapter(0, 0, 1)
-        load_frames(0, 1)
+        load_words(0)
         for q in range(4):
-            load_scale_rows(nc.sync, as_first, a_scales[:, :, 0:128], q)
+            load_scale_rows(nc.sync, as_first[:].bitcast(I32), a_scales[:, 0:1, :], q)
         for q in range(4):
             load_scale_rows(nc.sync if q % 2 == 0 else nc.gpsimd, xs[:].bitcast(I32), x_rows, q)
-        nc.gpsimd.dma_start(
-            out=vec[0:4, :].rearrange("t (n r) -> t n r", r=8),
-            in_=adapter_bias.rearrange("(n t r) -> t n r", t=4, r=8),
-        )
-        nc.gpsimd.dma_start(out=vec[32:48, 0:P], in_=proj_bias.rearrange("(i p) -> i p", p=P))
-        nc.gpsimd.dma_start(out=vec[64:80, 0:P], in_=feature_gain.rearrange("(i p) -> i p", p=P))
-        make_identity(nc, ident[:])
-        load_adapter(0, 1, KP)
-        load_frames(1, 2)
-        load_frames(2, KP)
-        load_adapter(1, 0, KP)
+        load_words(1)
         for q in range(4):
-            load_scale_rows(nc.sync, as_rest, a_scales[:, :, 128:384], q)
+            load_scale_rows(nc.sync, as_rest[:].bitcast(I32), a_scales[:, 1:KP, :], q)
+        nc.gpsimd.dma_start(out=abias[:], in_=adapter_bias.rearrange("(h p t) -> p h t", p=P, t=4))
+        nc.gpsimd.dma_start(out=vec[32:48, :], in_=proj_bias.rearrange("(i p) -> i p", p=P))
+        nc.gpsimd.dma_start(out=vec[64:80, :], in_=feature_gain.rearrange("(i p) -> i p", p=P))
+        make_identity(nc, ident[:])
+        load_words(2)
+        load_words(3)
         load_proj(0, 0)
-        load_adapter(2, 0, KP)
+        nc.sync.dma_start(out=aw_late[:].bitcast(I32), in_=a_codes[:, :, 512:768])
         load_proj(0, 1)
         nc.sync.dma_start(out=xw[1][:].bitcast(I32), in_=x_codes[:, :, 512:T])
         load_proj(0, 2)
@@ -179,10 +187,10 @@ def tile_speech_adapter_to_language_h2_kernel(
         load_te(1)
         load_proj(1, 2)
 
-        permute_words(0, 0, 1)
-        permute_scales(0)
-        permute_words(0, 1, KP)
-        nc.vector.tensor_copy(out=vec32[:], in_=vec[:])
+        for g in range(KP):
+            for h in range(2):
+                permute_words(h, g)
+                permute_scales(h, g)
 
         def adapter_pass(acc, s, g, t0, n, col):
             nc.tensor.matmul_mx(
@@ -202,7 +210,7 @@ def tile_speech_adapter_to_language_h2_kernel(
             if s % 4 == 0:
                 hrelu[grp, s // 4] = work.tile([P, 4, n], BF16, name="hrelu", tag="hrelu", bufs=2)
             nc.scalar.activation(
-                out=hrelu[grp, s // 4][:, s % 4, :], in_=acc[:, 0:n], func=ACT.Relu, bias=consts[:, P * (s // 4) + s % 4 : P * (s // 4) + s % 4 + 1]
+                out=hrelu[grp, s // 4][:, s % 4, :], in_=acc[:, 0:n], func=ACT.Relu, bias=abias[:, s // 4, s % 4 : s % 4 + 1]
             )
 
         inter = {}
@@ -232,10 +240,16 @@ def tile_speech_adapter_to_language_h2_kernel(
                 interleave(nc.scalar.copy, ("p", a, b), praw[a // 2, b][:, :, 512 * (a % 2) : 512 * (a % 2 + 1)], 0, 256)
             elif kind == "ps1":
                 interleave(nc.scalar.copy, ("p", a, b), praw[a // 2, b][:, :, 512 * (a % 2) : 512 * (a % 2 + 1)], 256, 512)
+            elif kind == "hs":
+                interleave(nc.scalar.copy, ("h", a, b), hrelu[a, b], 0, GROUPS[a][1])
+            elif kind in ("cv", "cs", "cg"):
+                round_rows(a, b, kind[1])
+            elif kind == "yq":
+                planes(a)
             elif kind == "aw":
-                permute_words(a, 0, KP)
+                permute_words(a, b)
             elif kind == "as":
-                permute_scales(a)
+                permute_scales(a, b)
             else:
                 cols = slice(512 * a, 512 * (a + 1))
                 quantize(("p", a, b), pw[:, b, cols], ps[:, b, cols])
@@ -248,13 +262,8 @@ def tile_speech_adapter_to_language_h2_kernel(
         for g in range(KP - 1):
             for s in range(EARLY):
                 adapter_pass(first[s], s, g, 0, 512, 0)
-        turned = bank(BANKS - 1)
-        for h in range(FP):
-            nc.tensor.transpose(turned[:, P * h : P * (h + 1)], vec32[:, P * h : P * (h + 1)], ident[:])
+        nc.vector.tensor_copy(out=vec32[:], in_=vec[:])
         fill(0, 0)
-        nc.vector.tensor_copy(out=consts[:], in_=turned[:, 0 : FP * P])
-        nc.vector.tensor_tensor(out=bias_gain[:], in0=consts[:, 32:48], in1=consts[:, 64:80], op=ALU.mult)
-
         for n in range(2 * SLOTS):
             grp, s = divmod(n, SLOTS)
             if n < EARLY:
@@ -265,11 +274,16 @@ def tile_speech_adapter_to_language_h2_kernel(
                 for g in range(KP):
                     adapter_pass(acc, s, g, 0, 512, 0)
             else:
-                acc = bank(n % BANKS)
+                acc = bank((n + 1) % BANKS)
                 for half in range(2):
                     for g in range(KP):
                         adapter_pass(acc, s, g, 512 + P * half, P, P * half)
             relu(acc, grp, s)
+            if n == SLOTS - 1:
+                turned = bank((n + 1) % BANKS)
+                nc.tensor.transpose(turned[:, 0:P], vec32[:], ident[:])
+                nc.scalar.copy(out=consts[:], in_=turned[:, 0:P])
+                nc.vector.tensor_tensor(out=bias_gain[:], in0=consts[:, 32:48], in1=consts[:, 64:80], op=ALU.mult)
             fill(1, n)
 
         units = [(c, t0, n) for c in range(CHUNKS) for (t0, n) in (GROUPS if c < CHUNKS - 1 else TAIL)]
@@ -285,7 +299,7 @@ def tile_speech_adapter_to_language_h2_kernel(
             c, t0, n = units[u]
             zg[u] = work.tile([P, 4, n], F32, name="zg", tag="zg", bufs=2, align_bytes=64)
             for i in range(4):
-                acc = next_bank("z", 0, 3)
+                acc = next_bank("z", 1, 3)
                 cols = slice(512 * c + P * i, 512 * c + P * (i + 1))
                 for g in range(FP):
                     nc.tensor.matmul_mx(
@@ -310,7 +324,7 @@ def tile_speech_adapter_to_language_h2_kernel(
                 nj = min(2, n // P - j0)
                 y[u, j0] = work.tile([P, nj, 512], F32, name="y", tag="y", bufs=6)
                 for j in range(j0, j0 + nj):
-                    acc = next_bank("y", 3, 4)
+                    acc = next_bank("y", 4, 4)
                     for i in range(4):
                         nc.tensor.transpose(acc[:, P * i : P * (i + 1)], zg[u][:, i, P * j : P * (j + 1)], ident[:])
                     nc.vector.tensor_tensor(
@@ -320,17 +334,18 @@ def tile_speech_adapter_to_language_h2_kernel(
                 nc.sync.dma_start(
                     out=out_0[rows, 512 * c : 512 * (c + 1)].rearrange("(j p) d -> p j d", p=P), in_=y[u, j0][:]
                 )
+                fill(2, u, 2, j0)
 
-        def round_rows(u, j0):
+        def round_rows(u, j0, engine):
             n = units[u][2]
             j1 = min(j0 + 2, n // P)
             if j0 == 0:
                 yb[u] = work.tile([P, n // P, 512], BF16, name="yb", tag="yb", bufs=2, align_bytes=64)
             out = yb[u][:, j0:j1, :].rearrange("p j (v m e) -> p j v m e", v=2, e=2)
             rows = y[u, j0][:].rearrange("p j (m v e) -> p j v m e", v=2, e=2)
-            if CAST[u] == "v":
+            if engine == "v":
                 nc.vector.tensor_copy(out=out, in_=rows)
-            elif CAST[u] == "s":
+            elif engine == "s":
                 nc.scalar.copy(out=out, in_=rows)
             else:
                 for j in range(j1 - j0):
@@ -341,7 +356,7 @@ def tile_speech_adapter_to_language_h2_kernel(
             if j0 == 0:
                 yi[u] = work.tile([P, n, 4], BF16, name="yi", tag="yi", bufs=2, align_bytes=64)
             pairs = yb[u][:].bitcast(F32)
-            acc = bank(BANKS - 1)
+            acc = bank(0)
             nj = min(2, n // P - j0)
             for jj in range(nj):
                 for v in range(2):
@@ -361,12 +376,14 @@ def tile_speech_adapter_to_language_h2_kernel(
             nc.sync.dma_start(
                 out=out_1[c].rearrange("p n t -> p (n t)").bitcast(I32)[:, t0 : t0 + n], in_=yw[:].bitcast(I32)
             )
+            if u == 2 * CHUNKS - 3:
+                store_scales(0, CHUNKS - 1)
 
         def store_scales(c0, c1):
             for q in range(4):
                 nc.sync.dma_start(
-                    out=out_2[c0:c1, 4 * q : 4 * q + 4, :].rearrange("g r n -> r g n").bitcast(I32),
-                    in_=ysc[32 * q : 32 * q + 4, c0:c1, :].bitcast(I32),
+                    out=out_2[c0:c1, q:16:4, :].rearrange("g r n -> r g n").bitcast(I32),
+                    in_=ysc[q:P:32, c0:c1, :].bitcast(I32),
                 )
 
         last = len(units) - 1
@@ -385,13 +402,4 @@ def tile_speech_adapter_to_language_h2_kernel(
             if u >= 1:
                 turn_words(u - 1, 2 if wide else 0)
             fill(2, u, 1, 1)
-            if u <= last:
-                round_rows(u, 0)
-            if u >= 1:
-                planes(u - 1)
-            if u <= last and units[u][2] == 512:
-                round_rows(u, 2)
-            fill(2, u, 1, 2)
-            if u == 2 * CHUNKS - 2:
-                store_scales(0, CHUNKS - 1)
         store_scales(CHUNKS - 1, CHUNKS)

@@ -17,66 +17,79 @@ ACT = mybir.ActivationFunctionType
 ALU = mybir.AluOpType
 
 P = 128
-KP = K // 512
-FP = F // 512
-SLOTS = 4 * FP
-CHUNKS = D // 512
+PACK = 4
+PASS = P * PACK
+K_PASSES = K // PASS
+F_PASSES = F // PASS
+F_TILES = F // P
+CHUNKS = D // PASS
 GROUPS = ((0, 512), (512, 256))
 BANKS = 8
-EARLY = 8
-CAST = "v"
-FILL = {
-    (0, 0): [("as", 2, 0), ("pv", 0, 0), ("as", 2, 2), ("ps0", 1, 0), ("ps1", 1, 0), ("as", 2, 1), ("aw", 2, 0)],
-    (1, 0): [("aw", 2, 2)],
-    (1, 1): [("aw", 2, 1), ("aw", 2, 3)],
-    (1, 2): [("pq", 1, 0)],
-    (1, 3): [("as", 2, 3)],
-    (1, 4): [("hi", 0, 0)],
-    (1, 6): [("pq", 0, 0)],
-    (1, 7): [("hq", 0, 0)],
-    (1, 9): [("hi", 0, 1), ("pv", 1, 2)],
-    (1, 10): [("pq", 1, 2), ("hq", 0, 1)],
-    (1, 11): [("ps0", 0, 1)],
-    (1, 12): [("ps1", 0, 1), ("hi", 0, 2)],
-    (1, 13): [("pv", 1, 1)],
-    (1, 15): [("pq", 0, 1), ("hq", 0, 2)],
-    (1, 19): [("hs", 1, 0), ("pv", 0, 2)],
-    (1, 22): [("pq", 1, 1), ("pq", 0, 2)],
-    (1, 23): [("hs", 1, 1), ("hi", 1, 2)],
-    (2, 0, 0, 0): [("hq", 1, 0)],
-    (2, 0, 0, 3): [("hq", 1, 2), ("hq", 1, 1), ("pv", 2, 2), ("pv", 2, 0)],
-    (2, 1, 0, 0): [("ps0", 3, 0)],
-    (2, 0, 1, 0): [("pv", 3, 1)],
-    (2, 0, 2, 0): [("pq", 2, 2)],
-    (2, 0, 2, 2): [("cv", 0, 0), ("ps1", 3, 0)],
-    (2, 2, 0, 0): [("pq", 2, 0)],
-    (2, 2, 0, 2): [("cv", 0, 2)],
-    (2, 1, 1, 0): [("pv", 2, 1)],
-    (2, 1, 2, 0): [("pq", 3, 1)],
-    (2, 3, 0, 1): [("cs", 1, 0)],
-    (2, 3, 0, 3): [("pq", 2, 1)],
-    (2, 2, 2, 2): [("yq", 0, 0)],
-    (2, 2, 1, 1): [("cs", 2, 0), ("yq", 1, 0), ("pv", 3, 2)],
-    (2, 4, 0, 1): [("cv", 2, 2)],
-    (2, 5, 0, 0): [("cs", 3, 0)],
-    (2, 5, 0, 1): [("pq", 3, 0)],
-    (2, 5, 0, 3): [("pq", 3, 2)],
-    (2, 4, 1, 0): [("yq", 2, 0)],
-    (2, 4, 2, 0): [("cv", 4, 0)],
-    (2, 6, 0, 3): [("cv", 4, 2)],
-    (2, 5, 2, 0): [("yq", 3, 0)],
-    (2, 5, 1, 1): [("yq", 4, 0)],
-    (2, 7, 0, 1): [("cv", 5, 0)],
-    (2, 8, 0, 0): [("yq", 5, 0)],
-    (2, 8, 0, 2): [("cv", 6, 0)],
-    (2, 9, 0, 1): [("cv", 7, 0)],
-    (2, 9, 0, 3): [("yq", 6, 0)],
-    (2, 9, 1, 0): [("cs", 8, 0)],
-    (2, 9, 1, 1): [("cv", 9, 0), ("yq", 7, 0)],
-    (2, 10, 1, 0): [("yq", 8, 0)],
-    (2, 10, 1, 1): [("yq", 9, 0)],
+BIAS_ROW, GAIN_ROW = 32, 64
+
+UNITS = [(c, t0, n) for c in range(CHUNKS) for (t0, n) in GROUPS]
+LAST = len(UNITS) - 1
+
+Z_BANKS, Y_BANKS, PAIR_BANKS, PAIR_BANKS_AT_END = (1, 3), (4, 4), (0, 1), (0, 4)
+
+VECTOR, SCALAR = "vector", "scalar"
+
+JOBS_AFTER = {
+    ("opening",): [("mix_proj", VECTOR, 1, 0, 0, 512)],
+    ("adapter", 2): [("mix_proj", VECTOR, 0, 0, 0, 512)],
+    ("adapter", 3): [("quantize_proj", 1, 0)],
+    ("adapter", 4): [("mix_h", SCALAR, 0, 0), ("quantize_proj", 0, 0)],
+    ("adapter", 5): [("mix_proj", VECTOR, 0, 1, 0, 512)],
+    ("adapter", 6): [("quantize_h", 0, 0)],
+    ("adapter", 8): [("quantize_proj", 0, 1), ("mix_h", VECTOR, 0, 1)],
+    ("adapter", 11): [("mix_proj", VECTOR, 0, 2, 0, 512), ("mix_h", SCALAR, 0, 2)],
+    ("adapter", 16): [("mix_h", SCALAR, 1, 0), ("quantize_h", 0, 1)],
+    ("adapter", 17): [("quantize_proj", 0, 2), ("mix_proj", VECTOR, 1, 2, 0, 512), ("quantize_h", 1, 0)],
+    ("adapter", 20): [("quantize_h", 0, 2)],
+    ("adapter", 22): [("mix_proj", VECTOR, 1, 1, 0, 512), ("mix_h", SCALAR, 1, 1)],
+    ("project", 0, 0): [("quantize_proj", 1, 2), ("quantize_proj", 1, 1)],
+    ("project", 0, 1): [("mix_h", VECTOR, 1, 2)],
+    ("project", 0, 3): [("quantize_h", 1, 1), ("quantize_h", 1, 2)],
+    ("project", 1, 0): [("mix_proj", VECTOR, 2, 1, 0, 512), ("mix_proj", VECTOR, 3, 0, 0, 512)],
+    ("project", 1, 1): [("mix_proj", SCALAR, 2, 0, 0, 256)],
+    ("project", 1, 2): [("mix_proj", VECTOR, 2, 2, 0, 512)],
+    ("before_turn", 0): [("mix_proj", SCALAR, 2, 0, 256, 512)],
+    ("after_turn", 0): [("round_y", VECTOR, 0, 0), ("quantize_proj", 2, 1)],
+    ("project", 2, 2): [("quantize_proj", 2, 0)],
+    ("stored", 1, 0): [("turn_y", SCALAR, 0, 0)],
+    ("after_turn", 1): [("quantize_proj", 3, 0)],
+    ("project", 3, 0): [("quantize_proj", 2, 2)],
+    ("project", 3, 1): [("round_y", SCALAR, 0, 2)],
+    ("project", 3, 3): [("round_y", SCALAR, 1, 0), ("mix_proj", VECTOR, 3, 2, 0, 512)],
+    ("after_turn", 2): [("turn_y", SCALAR, 0, 2)],
+    ("project", 4, 2): [("round_y", VECTOR, 2, 0)],
+    ("before_turn", 3): [("round_y", VECTOR, 2, 2)],
+    ("stored", 3, 0): [("quantize_y", 0, 0), ("turn_y", SCALAR, 2, 0)],
+    ("after_turn", 3): [("mix_proj", VECTOR, 3, 1, 0, 512)],
+    ("project", 5, 1): [("quantize_proj", 3, 2)],
+    ("project", 5, 3): [("quantize_proj", 3, 1)],
+    ("before_turn", 4): [("turn_y", SCALAR, 1, 0), ("quantize_y", 1, 0)],
+    ("stored", 4, 2): [("round_y", VECTOR, 3, 0), ("turn_y", SCALAR, 2, 2)],
+    ("project", 6, 0): [("round_y", SCALAR, 4, 0)],
+    ("project", 6, 1): [("quantize_y", 2, 0)],
+    ("after_turn", 5): [("turn_y", VECTOR, 3, 0), ("round_y", VECTOR, 5, 0)],
+    ("project", 7, 0): [("quantize_y", 3, 0)],
+    ("project", 7, 2): [("round_y", SCALAR, 4, 2)],
+    ("stored", 6, 0): [("turn_y", SCALAR, 5, 0)],
+    ("after_turn", 6): [("turn_y", SCALAR, 4, 0), ("turn_y", VECTOR, 4, 2), ("quantize_y", 4, 0)],
+    ("before_turn", 7): [("round_y", SCALAR, 6, 0), ("quantize_y", 5, 0)],
+    ("added", 7, 0): [("round_y", SCALAR, 6, 2)],
+    ("added", 7, 1): [("turn_y", SCALAR, 6, 0), ("round_y", SCALAR, 7, 0)],
+    ("after_turn", 7): [
+        ("turn_y", VECTOR, 6, 2),
+        ("round_y", VECTOR, 7, 1),
+        ("turn_y", SCALAR, 7, 0),
+        ("quantize_y", 6, 0),
+        ("turn_y", SCALAR, 7, 1),
+        ("quantize_y", 7, 1),
+        ("quantize_y", 7, 0),
+    ],
 }
-TAIL = ((0, 256), (256, 256), (512, 128), (640, 128))
 
 
 def tile_speech_adapter_to_language_h2_kernel(
@@ -84,6 +97,7 @@ def tile_speech_adapter_to_language_h2_kernel(
     feature_gain, time_embed, out_0, out_1, out_2,
 ):
     nc = tc.nc
+    copy_on = {VECTOR: nc.vector.tensor_copy, SCALAR: nc.scalar.copy}
     with ExitStack() as ctx:
         keep = ctx.enter_context(tc.tile_pool(name="keep", bufs=1))
         work = ctx.enter_context(tc.tile_pool(name="work", bufs=2))
@@ -91,315 +105,310 @@ def tile_speech_adapter_to_language_h2_kernel(
         ctx.enter_context(tc.manual_schedule())
 
         def bank(n):
-            return psum.tile([P, 512], F32, name="bank%d" % n, tag="bank%d" % n)
+            return psum.tile([P, PASS], F32, name="bank%d" % n, tag="bank%d" % n)
 
-        xw = [keep.tile([P, KP, n], U32, name="xw%d" % t0, align_bytes=64) for (t0, n) in GROUPS]
-        xs = keep.tile([P, KP, T], U8, name="xs", align_bytes=64)
-        aw = keep.tile([P, FP, KP, 1024], U8, name="aw", align_bytes=64)
-        asc = keep.tile([P, FP, KP, 512], U8, name="asc", align_bytes=64)
-        aw_early = work.tile([P, KP, 2048], U8, name="aw_early", tag="zg", bufs=2, align_bytes=64)
-        aw_late = work.tile([P, KP, 1024], U8, name="aw_late", tag="yi", bufs=2, align_bytes=64)
-        as_first = work.tile([P, 1, F], U8, name="as_first", tag="yi", bufs=2, align_bytes=64)
-        as_rest = work.tile([P, KP - 1, F], U8, name="as_rest", tag="zg", bufs=2, align_bytes=64)
-        pw = keep.tile([P, FP, D], U32, name="pw", align_bytes=64)
-        ps = keep.tile([P, FP, D], U8, name="ps", align_bytes=64)
-        hw = keep.tile([P, FP, T], U32, name="hw", align_bytes=64)
-        hs = keep.tile([P, FP, T], U8, name="hs", align_bytes=64)
-        ysc = keep.tile([P, CHUNKS, T], U8, name="ysc", align_bytes=64)
-        abias = keep.tile([P, FP, 4], BF16, name="abias")
-        vec = keep.tile([P, P], BF16, name="vec")
-        vec32 = keep.tile([P, P], F32, name="vec32")
+        x_codes = [keep.tile([P, K_PASSES, n], U32, name="x_codes%d" % t0, align_bytes=64) for (t0, n) in GROUPS]
+        x_plane = keep.tile([P, K_PASSES, T], U8, name="x_plane", align_bytes=64)
+        a_codes = [
+            work.tile([P, K_PASSES, 2 * PASS], U8, name="a_codes%d" % h, tag="y", bufs=9, align_bytes=64)
+            for h in range(F_PASSES)
+        ]
+        a_plane = keep.tile([P, F_PASSES, K_PASSES, PASS], U8, name="a_plane", align_bytes=64)
+        a_raw_early = work.tile([P, K_PASSES, 4 * PASS], U8, name="a_raw_early", tag="zg", bufs=2, align_bytes=64)
+        a_raw_late = work.tile([P, K_PASSES, 2 * PASS], U8, name="a_raw_late", tag="y_mixed", bufs=2, align_bytes=64)
+        a_rows_first = work.tile([P, 1, F], U8, name="a_rows_first", tag="y_mixed", bufs=2, align_bytes=64)
+        a_rows_rest = work.tile([P, K_PASSES - 1, F], U8, name="a_rows_rest", tag="zg", bufs=2, align_bytes=64)
+        p_codes = keep.tile([P, F_PASSES, D], U32, name="p_codes", align_bytes=64)
+        p_plane = keep.tile([P, F_PASSES, D], U8, name="p_plane", align_bytes=64)
+        h_codes = keep.tile([P, F_PASSES, T], U32, name="h_codes", align_bytes=64)
+        h_plane = keep.tile([P, F_PASSES, T], U8, name="h_plane", align_bytes=64)
+        y_plane = keep.tile([P, CHUNKS, T], U8, name="y_plane", align_bytes=64)
+        a_bias = keep.tile([P, F_PASSES, PACK], BF16, name="a_bias")
+        staged = keep.tile([P, P], BF16, name="staged")
+        staged32 = keep.tile([P, P], F32, name="staged32")
         ident = keep.tile([P, P], F32, name="ident")
-        consts = keep.tile([P, P], F32, name="consts")
-        bias_gain = keep.tile([P, 16], F32, name="bias_gain")
-        warm = keep.tile([P, 8], F32, name="warm")
+        by_feature = keep.tile([P, P], F32, name="by_feature")
+        bias_gain = keep.tile([P, D // P], F32, name="bias_gain")
 
-        x_codes = x_words.rearrange("g p n t -> p g (n t)").bitcast(I32)
-        a_codes = adapter_words.rearrange("g p n -> p g n").bitcast(I32)
-
-        a_scales = adapter_scales.rearrange("g q n -> q g n").bitcast(I32)
-        x_rows = x_scales.rearrange("g q n -> q g n").bitcast(I32)
-        proj_rows = proj.rearrange("(h p t) d -> h p t d", h=FP, t=4)
-        praw = {}
-        te = {}
+        x_words32 = x_words.rearrange("g p n t -> p g (n t)").bitcast(I32)
+        a_words32 = adapter_words.rearrange("g p n -> p g n").bitcast(I32)
+        a_scales32 = adapter_scales.rearrange("g q n -> q g n").bitcast(I32)
+        x_scales32 = x_scales.rearrange("g q n -> q g n").bitcast(I32)
+        proj_rows = proj.rearrange("(h p t) d -> h p t d", h=F_PASSES, t=PACK)
+        p_raw = {}
+        embed = {}
 
         def load_words(g):
-            nc.sync.dma_start(out=aw_early[:, g, :].bitcast(I32), in_=a_codes[:, g, 0:512])
-            nc.sync.dma_start(out=xw[0][:, g, :].bitcast(I32), in_=x_codes[:, g, 0:512])
+            nc.sync.dma_start(out=a_raw_early[:, g, :].bitcast(I32), in_=a_words32[:, g, 0:PASS])
+            nc.sync.dma_start(out=x_codes[0][:, g, :].bitcast(I32), in_=x_words32[:, g, 0:PASS])
 
-        def load_scale_rows(queue, plane, rows, q):
-            queue.dma_start(out=plane[q:P:32, :, :], in_=rows[q:16:4, :, :])
+        def load_scale_rows(plane, rows):
+            for r in range(4):
+                nc.sync.dma_start(out=plane[:].bitcast(I32)[r:P:32, :, :], in_=rows[r:16:4, :, :])
 
         def load_proj(half, h):
-            praw[half, h] = work.tile([P, 4, 1024], BF16, name="praw%d%d" % (half, h), tag="praw", bufs=2 * FP)
-            nc.sync.dma_start(out=praw[half, h][:], in_=proj_rows[h][:, :, 1024 * half : 1024 * (half + 1)])
-
-        def load_te(c):
-            if c < 2:
-                te[c] = keep.tile([P, T // P, 512], BF16, name="te%d" % c)
-            else:
-                te[c] = work.tile([P, T // P, 512], BF16, name="te%d" % c, tag="praw", bufs=2 * FP)
-            nc.sync.dma_start(
-                out=te[c][:], in_=time_embed[:, 512 * c : 512 * (c + 1)].rearrange("(j p) d -> p j d", p=P)
+            p_raw[half, h] = work.tile(
+                [P, PACK, 2 * PASS], BF16, name="p_raw%d%d" % (half, h), tag="p_raw", bufs=2 * F_PASSES
             )
+            cols = slice(2 * PASS * half, 2 * PASS * (half + 1))
+            nc.sync.dma_start(out=p_raw[half, h][:], in_=proj_rows[h][:, :, cols])
 
-        def permute_words(h, g):
-            rows = aw_early[:, g, 1024 * h : 1024 * (h + 1)] if h < 2 else aw_late[:, g, :]
-            nc.vector.tensor_copy(
-                out=aw[:, h, g, :].rearrange("p (t m e) -> p t m e", t=4, e=2),
-                in_=rows.rearrange("p (m t e) -> p t m e", t=4, e=2),
-            )
+        def load_embed(c, tile):
+            embed[c] = tile
+            cols = slice(PASS * c, PASS * (c + 1))
+            nc.sync.dma_start(out=tile[:], in_=time_embed[:, cols].rearrange("(j p) d -> p j d", p=P))
 
-        def permute_scales(h, g):
-            rows = (as_first[:, 0, :] if g == 0 else as_rest[:, g - 1, :])[:, 512 * h : 512 * (h + 1)]
-            nc.vector.tensor_copy(
-                out=asc[:, h, g, :].rearrange("p (t m) -> p t m", t=4), in_=rows.rearrange("p (m t) -> p t m", t=4)
-            )
-
-        nc.vector.memset(as_first[:].bitcast(I32), 0)
-        nc.gpsimd.memset(xs[:].bitcast(I32), 0)
-        nc.vector.memset(as_rest[:].bitcast(I32), 0)
-        nc.vector.memset(vec[:], 0.0)
-        nc.vector.memset(warm[:], 0.0)
-        nc.scalar.activation(out=warm[:, 0:1], in_=warm[:, 4:5], func=ACT.Relu)
-        load_words(0)
-        for q in range(4):
-            load_scale_rows(nc.sync, as_first[:].bitcast(I32), a_scales[:, 0:1, :], q)
-        for q in range(4):
-            load_scale_rows(nc.sync if q % 2 == 0 else nc.gpsimd, xs[:].bitcast(I32), x_rows, q)
-        load_words(1)
-        for q in range(4):
-            load_scale_rows(nc.sync, as_rest[:].bitcast(I32), a_scales[:, 1:KP, :], q)
-        nc.gpsimd.dma_start(out=abias[:], in_=adapter_bias.rearrange("(h p t) -> p h t", p=P, t=4))
-        nc.gpsimd.dma_start(out=vec[32:48, :], in_=proj_bias.rearrange("(i p) -> i p", p=P))
-        nc.gpsimd.dma_start(out=vec[64:80, :], in_=feature_gain.rearrange("(i p) -> i p", p=P))
+        nc.vector.memset(a_rows_first[:].bitcast(I32), 0)
+        nc.vector.memset(x_plane[:].bitcast(I32), 0)
+        nc.vector.memset(a_rows_rest[:].bitcast(I32), 0)
+        nc.vector.memset(staged[:], 0.0)
         make_identity(nc, ident[:])
+        load_words(0)
+        load_scale_rows(a_rows_first, a_scales32[:, 0:1, :])
+        load_scale_rows(x_plane, x_scales32)
+        load_scale_rows(a_rows_rest, a_scales32[:, 1:K_PASSES, :])
+        load_words(1)
+        nc.sync.dma_start(out=a_bias[:], in_=adapter_bias.rearrange("(h p t) -> p h t", p=P, t=PACK))
+        nc.sync.dma_start(out=staged[BIAS_ROW : BIAS_ROW + 16, :], in_=proj_bias.rearrange("(m p) -> m p", p=P))
+        nc.sync.dma_start(out=staged[GAIN_ROW : GAIN_ROW + 16, :], in_=feature_gain.rearrange("(m p) -> m p", p=P))
         load_words(2)
         load_words(3)
+        nc.sync.dma_start(out=a_raw_late[:].bitcast(I32), in_=a_words32[:, :, PASS : F // 2])
         load_proj(0, 0)
-        nc.sync.dma_start(out=aw_late[:].bitcast(I32), in_=a_codes[:, :, 512:768])
         load_proj(0, 1)
-        nc.sync.dma_start(out=xw[1][:].bitcast(I32), in_=x_codes[:, :, 512:T])
+        nc.sync.dma_start(out=x_codes[1][:].bitcast(I32), in_=x_words32[:, :, PASS:T])
         load_proj(0, 2)
         load_proj(1, 0)
-        load_te(0)
+        load_embed(0, keep.tile([P, T // P, PASS], BF16, name="embed0"))
         load_proj(1, 1)
-        load_te(1)
+        load_embed(1, keep.tile([P, T // P, PASS], BF16, name="embed1"))
         load_proj(1, 2)
 
-        for g in range(KP):
+        def reorder_words(h, g):
+            raw = a_raw_early[:, g, 2 * PASS * h : 2 * PASS * (h + 1)] if h < 2 else a_raw_late[:, g, :]
+            nc.vector.tensor_copy(
+                out=a_codes[h][:, g, :].rearrange("p (t m e) -> p t m e", t=PACK, e=2),
+                in_=raw.rearrange("p (m t e) -> p t m e", t=PACK, e=2),
+            )
+
+        def reorder_scales(h, g):
+            raw = (a_rows_first[:, 0, :] if g == 0 else a_rows_rest[:, g - 1, :])[:, PASS * h : PASS * (h + 1)]
+            nc.vector.tensor_copy(
+                out=a_plane[:, h, g, :].rearrange("p (t m) -> p t m", t=PACK),
+                in_=raw.rearrange("p (m t) -> p t m", t=PACK),
+            )
+
+        for h in range(2):
+            reorder_words(h, 0)
+        for h in range(F_PASSES):
+            reorder_scales(h, 0)
+        for h in range(2):
+            reorder_scales(h, 1)
+        for h in range(2):
+            reorder_words(h, 1)
+        for g in (2, 3):
             for h in range(2):
-                permute_words(h, g)
-                permute_scales(h, g)
+                reorder_scales(h, g)
+            reorder_words(0, g)
+        for g in (2, 3):
+            reorder_words(1, g)
+        for g in range(1, K_PASSES):
+            reorder_scales(2, g)
+        for g in range(K_PASSES):
+            reorder_words(2, g)
 
-        def adapter_pass(acc, s, g, t0, n, col):
-            nc.tensor.matmul_mx(
-                out=acc[:, col : col + n],
-                lhsT=aw[:, s // 4, g, 256 * (s % 4) : 256 * (s % 4 + 1)].bitcast(FP4X4),
-                lhsT_scale=asc[:, s // 4, g, P * (s % 4) : P * (s % 4 + 1)],
-                rhs=xw[t0 // 512][:, g, t0 % 512 : t0 % 512 + n].bitcast(FP8X4),
-                rhs_scale=xs[:, g, t0 : t0 + n],
-                start=(g == 0),
-                stop=(g == KP - 1),
-            )
+        h_rows, mixed, zg, y, y_pairs, y_mixed = {}, {}, {}, {}, {}, {}
+        banks_taken = {}
 
-        hrelu = {}
+        def next_bank(banks):
+            first, count = banks
+            taken = banks_taken.get(banks, 0)
+            banks_taken[banks] = taken + 1
+            return bank(first + taken % count)
 
-        def relu(acc, grp, s):
-            n = GROUPS[grp][1]
-            if s % 4 == 0:
-                hrelu[grp, s // 4] = work.tile([P, 4, n], BF16, name="hrelu", tag="hrelu", bufs=2)
-            nc.scalar.activation(
-                out=hrelu[grp, s // 4][:, s % 4, :], in_=acc[:, 0:n], func=ACT.Relu, bias=abias[:, s // 4, s % 4 : s % 4 + 1]
-            )
-
-        inter = {}
-
-        def interleave(engine_copy, key, rows, c0, c1):
+        def mix(engine, key, rows, c0, c1):
             if c0 == 0:
-                inter[key] = work.tile([P, rows.shape[2], 4], BF16, name="inter", tag="inter", bufs=4, align_bytes=64)
-            engine_copy(
-                out=inter[key][:, c0:c1, :].rearrange("p (c i) t -> p c t i", i=4),
+                mixed[key] = work.tile(
+                    [P, rows.shape[2], PACK], BF16, name="mixed", tag="mixed", bufs=4, align_bytes=64
+                )
+            copy_on[engine](
+                out=mixed[key][:, c0:c1, :].rearrange("p (c i) t -> p c t i", i=4),
                 in_=rows[:, :, c0:c1].rearrange("p t (c i) -> p c t i", i=4),
             )
 
-        def quantize(key, words, scales):
-            nc.vector.quantize_mx(
-                out=words.bitcast(FP8X4), scales=scales, in_=inter[key][:].rearrange("p n t -> p (n t)")
+        def quantize(source, codes, plane):
+            nc.vector.quantize_mx(out=codes.bitcast(FP8X4), scales=plane, in_=source.rearrange("p n t -> p (n t)"))
+
+        def mix_proj(engine, c, h, c0, c1):
+            mix(engine, ("proj", c, h), p_raw[c // 2, h][:, :, PASS * (c % 2) : PASS * (c % 2 + 1)], c0, c1)
+
+        def quantize_proj(c, h):
+            cols = slice(PASS * c, PASS * (c + 1))
+            quantize(mixed["proj", c, h][:], p_codes[:, h, cols], p_plane[:, h, cols])
+
+        def mix_h(engine, group, h):
+            mix(engine, ("h", group, h), h_rows[group, h], 0, GROUPS[group][1])
+
+        def quantize_h(group, h):
+            t0, n = GROUPS[group]
+            quantize(mixed["h", group, h][:], h_codes[:, h, t0 : t0 + n], h_plane[:, h, t0 : t0 + n])
+
+        def frame_tiles(u):
+            return 1 if u == LAST else 2
+
+        def round_y(engine, u, j0):
+            n, nj = UNITS[u][2], frame_tiles(u)
+            if j0 == 0:
+                y_pairs[u] = work.tile([P, n // P, PASS], BF16, name="y_pairs", tag="y_pairs", bufs=3, align_bytes=64)
+            copy_on[engine](
+                out=y_pairs[u][:, j0 : j0 + nj, :].rearrange("p j (v m e) -> p j v m e", v=2, e=2),
+                in_=y[u, j0 - j0 % 2][:, j0 % 2 : j0 % 2 + nj, :].rearrange("p j (m v e) -> p j v m e", v=2, e=2),
             )
 
-        def job(kind, a, b):
-            if kind == "hi":
-                interleave(nc.vector.tensor_copy, ("h", a, b), hrelu[a, b], 0, GROUPS[a][1])
-            elif kind == "hq":
-                t0, n = GROUPS[a]
-                quantize(("h", a, b), hw[:, b, t0 : t0 + n], hs[:, b, t0 : t0 + n])
-            elif kind == "pv":
-                interleave(nc.vector.tensor_copy, ("p", a, b), praw[a // 2, b][:, :, 512 * (a % 2) : 512 * (a % 2 + 1)], 0, 512)
-            elif kind == "ps0":
-                interleave(nc.scalar.copy, ("p", a, b), praw[a // 2, b][:, :, 512 * (a % 2) : 512 * (a % 2 + 1)], 0, 256)
-            elif kind == "ps1":
-                interleave(nc.scalar.copy, ("p", a, b), praw[a // 2, b][:, :, 512 * (a % 2) : 512 * (a % 2 + 1)], 256, 512)
-            elif kind == "hs":
-                interleave(nc.scalar.copy, ("h", a, b), hrelu[a, b], 0, GROUPS[a][1])
-            elif kind in ("cv", "cs", "cg"):
-                round_rows(a, b, kind[1])
-            elif kind == "yq":
-                planes(a)
-            elif kind == "aw":
-                permute_words(a, b)
-            elif kind == "as":
-                permute_scales(a, b)
-            else:
-                cols = slice(512 * a, 512 * (a + 1))
-                quantize(("p", a, b), pw[:, b, cols], ps[:, b, cols])
-
-        def fill(*key):
-            for item in FILL.get(key, ()):
-                job(*item)
-
-        first = [bank(s) for s in range(EARLY)]
-        for g in range(KP - 1):
-            for s in range(EARLY):
-                adapter_pass(first[s], s, g, 0, 512, 0)
-        nc.vector.tensor_copy(out=vec32[:], in_=vec[:])
-        fill(0, 0)
-        for n in range(2 * SLOTS):
-            grp, s = divmod(n, SLOTS)
-            if n < EARLY:
-                acc = first[n]
-                adapter_pass(acc, s, KP - 1, 0, 512, 0)
-            elif grp == 0:
-                acc = bank(n % BANKS)
-                for g in range(KP):
-                    adapter_pass(acc, s, g, 0, 512, 0)
-            else:
-                acc = bank((n + 1) % BANKS)
-                for half in range(2):
-                    for g in range(KP):
-                        adapter_pass(acc, s, g, 512 + P * half, P, P * half)
-            relu(acc, grp, s)
-            if n == SLOTS - 1:
-                turned = bank((n + 1) % BANKS)
-                nc.tensor.transpose(turned[:, 0:P], vec32[:], ident[:])
-                nc.scalar.copy(out=consts[:], in_=turned[:, 0:P])
-                nc.vector.tensor_tensor(out=bias_gain[:], in0=consts[:, 32:48], in1=consts[:, 64:80], op=ALU.mult)
-            fill(1, n)
-
-        units = [(c, t0, n) for c in range(CHUNKS) for (t0, n) in (GROUPS if c < CHUNKS - 1 else TAIL)]
-        zg, y, yb, yi = {}, {}, {}, {}
-        count = {"z": 0, "y": 0, "w": 0}
-
-        def next_bank(role, base, depth):
-            n = base + count[role] % depth
-            count[role] += 1
-            return bank(n)
-
-        def project(u):
-            c, t0, n = units[u]
-            zg[u] = work.tile([P, 4, n], F32, name="zg", tag="zg", bufs=2, align_bytes=64)
-            for i in range(4):
-                acc = next_bank("z", 1, 3)
-                cols = slice(512 * c + P * i, 512 * c + P * (i + 1))
-                for g in range(FP):
-                    nc.tensor.matmul_mx(
-                        out=acc[:, 0:n],
-                        lhsT=pw[:, g, cols].bitcast(FP8X4),
-                        lhsT_scale=ps[:, g, cols],
-                        rhs=hw[:, g, t0 : t0 + n].bitcast(FP8X4),
-                        rhs_scale=hs[:, g, t0 : t0 + n],
-                        start=(g == 0),
-                        stop=(g == FP - 1),
-                    )
-                m = 4 * c + i
-                nc.scalar.activation(
-                    out=zg[u][:, i, :], in_=acc[:, 0:n], func=ACT.Identity,
-                    scale=consts[:, 64 + m : 65 + m], bias=bias_gain[:, m : m + 1],
-                )
-                fill(2, u, 0, i)
-
-        def turn_back(u):
-            c, t0, n = units[u]
-            for j0 in range(0, n // P, 2):
-                nj = min(2, n // P - j0)
-                y[u, j0] = work.tile([P, nj, 512], F32, name="y", tag="y", bufs=6)
-                for j in range(j0, j0 + nj):
-                    acc = next_bank("y", 4, 4)
-                    for i in range(4):
-                        nc.tensor.transpose(acc[:, P * i : P * (i + 1)], zg[u][:, i, P * j : P * (j + 1)], ident[:])
-                    nc.vector.tensor_tensor(
-                        out=y[u, j0][:, j - j0, :], in0=acc[:], in1=te[c][:, t0 // P + j, :], op=ALU.add
-                    )
-                rows = slice(t0 + P * j0, t0 + P * (j0 + nj))
-                nc.sync.dma_start(
-                    out=out_0[rows, 512 * c : 512 * (c + 1)].rearrange("(j p) d -> p j d", p=P), in_=y[u, j0][:]
-                )
-                fill(2, u, 2, j0)
-
-        def round_rows(u, j0, engine):
-            n = units[u][2]
-            j1 = min(j0 + 2, n // P)
+        def turn_y(engine, u, j0):
+            n, nj = UNITS[u][2], frame_tiles(u)
             if j0 == 0:
-                yb[u] = work.tile([P, n // P, 512], BF16, name="yb", tag="yb", bufs=2, align_bytes=64)
-            out = yb[u][:, j0:j1, :].rearrange("p j (v m e) -> p j v m e", v=2, e=2)
-            rows = y[u, j0][:].rearrange("p j (m v e) -> p j v m e", v=2, e=2)
-            if engine == "v":
-                nc.vector.tensor_copy(out=out, in_=rows)
-            elif engine == "s":
-                nc.scalar.copy(out=out, in_=rows)
-            else:
-                for j in range(j1 - j0):
-                    nc.gpsimd.tensor_scalar(out=out[:, j], in0=rows[:, j], scalar1=1.0, scalar2=0.0, op0=ALU.mult, op1=ALU.add)
-
-        def turn_words(u, j0):
-            n = units[u][2]
-            if j0 == 0:
-                yi[u] = work.tile([P, n, 4], BF16, name="yi", tag="yi", bufs=2, align_bytes=64)
-            pairs = yb[u][:].bitcast(F32)
-            acc = bank(0)
-            nj = min(2, n // P - j0)
+                y_mixed[u] = work.tile([P, n, PACK], BF16, name="y_mixed", tag="y_mixed", bufs=2, align_bytes=64)
+            pairs = y_pairs[u][:].bitcast(F32)
+            matmuls_done = banks_taken[Z_BANKS] == 4 * len(UNITS)
+            acc = next_bank(PAIR_BANKS_AT_END if matmuls_done else PAIR_BANKS)
             for jj in range(nj):
                 for v in range(2):
                     col = P * (2 * jj + v)
                     nc.tensor.transpose(acc[:, col : col + P], pairs[:, j0 + jj, P * v : P * (v + 1)], ident[:])
-            nc.scalar.copy(
-                out=yi[u][:, P * j0 : P * (j0 + nj), :].bitcast(F32).rearrange("p (j m) v -> p j m v", j=nj),
-                in_=acc[:, 0 : 256 * nj].rearrange("p (j v m) -> p j m v", j=nj, v=2),
+            copy_on[engine](
+                out=y_mixed[u][:, P * j0 : P * (j0 + nj), :].bitcast(F32).rearrange("p (j m) v -> p j m v", j=nj),
+                in_=acc[:, 0 : 2 * P * nj].rearrange("p (j v m) -> p j m v", j=nj, v=2),
             )
-
-        def planes(u):
-            c, t0, n = units[u]
-            yw = work.tile([P, n], U32, name="yw", tag="yw", bufs=3, align_bytes=64)
-            nc.vector.quantize_mx(
-                out=yw[:].bitcast(FP8X4), scales=ysc[:, c, t0 : t0 + n], in_=yi[u][:].rearrange("p n t -> p (n t)")
-            )
-            nc.sync.dma_start(
-                out=out_1[c].rearrange("p n t -> p (n t)").bitcast(I32)[:, t0 : t0 + n], in_=yw[:].bitcast(I32)
-            )
-            if u == 2 * CHUNKS - 3:
-                store_scales(0, CHUNKS - 1)
 
         def store_scales(c0, c1):
-            for q in range(4):
-                nc.sync.dma_start(
-                    out=out_2[c0:c1, q:16:4, :].rearrange("g r n -> r g n").bitcast(I32),
-                    in_=ysc[q:P:32, c0:c1, :].bitcast(I32),
+            for r in range(4):
+                queue = nc.scalar if c1 == CHUNKS and r % 2 else nc.sync
+                queue.dma_start(
+                    out=out_2[c0:c1, r:16:4, :].rearrange("g q n -> q g n").bitcast(I32),
+                    in_=y_plane[r:P:32, c0:c1, :].bitcast(I32),
                 )
 
-        last = len(units) - 1
-        load_te(2)
-        load_te(3)
+        def quantize_y(u, j0):
+            c, t0, n = UNITS[u]
+            m0, m1 = (P * j0, P * (j0 + 1)) if u == LAST else (0, n)
+            y_codes = work.tile([P, m1 - m0], U32, name="y_codes", tag="y_codes", bufs=3, align_bytes=64)
+            quantize(y_mixed[u][:, m0:m1, :], y_codes[:], y_plane[:, c, t0 + m0 : t0 + m1])
+            nc.sync.dma_start(
+                out=out_1[c].rearrange("p n t -> p (n t)").bitcast(I32)[:, t0 + m0 : t0 + m1],
+                in_=y_codes[:].bitcast(I32),
+            )
+            if u == LAST - len(GROUPS):
+                store_scales(0, CHUNKS - 1)
+
+        jobs = {
+            "mix_proj": mix_proj, "quantize_proj": quantize_proj, "mix_h": mix_h, "quantize_h": quantize_h,
+            "round_y": round_y, "turn_y": turn_y, "quantize_y": quantize_y,
+        }
+
+        def jobs_after(*step):
+            for job in JOBS_AFTER.get(step, ()):
+                jobs[job[0]](*job[1:])
+
+        def adapter_pass(acc, s, g, t0, n, col):
+            h, t = divmod(s, PACK)
+            nc.tensor.matmul_mx(
+                out=acc[:, col : col + n],
+                lhsT=a_codes[h][:, g, 2 * P * t : 2 * P * (t + 1)].bitcast(FP4X4),
+                lhsT_scale=a_plane[:, h, g, P * t : P * (t + 1)],
+                rhs=x_codes[t0 // PASS][:, g, t0 % PASS : t0 % PASS + n].bitcast(FP8X4),
+                rhs_scale=x_plane[:, g, t0 : t0 + n],
+                start=(g == 0),
+                stop=(g == K_PASSES - 1),
+            )
+
+        opened = [bank(s) for s in range(BANKS)]
+        for g in range(2):
+            for s in range(BANKS):
+                adapter_pass(opened[s], s, g, 0, PASS, 0)
+        nc.scalar.activation(out=staged32[:], in_=staged[:], func=ACT.Identity)
+        jobs_after("opening")
+        for step in range(2 * F_TILES):
+            group, s = divmod(step, F_TILES)
+            t0, n = GROUPS[group]
+            if step < BANKS:
+                acc = opened[step]
+                for g in range(2, K_PASSES):
+                    adapter_pass(acc, s, g, t0, n, 0)
+            elif group == 0:
+                acc = bank(step % BANKS)
+                for g in range(K_PASSES):
+                    adapter_pass(acc, s, g, t0, n, 0)
+            else:
+                acc = bank((step + 1) % BANKS)
+                for col in range(0, n, P):
+                    for g in range(K_PASSES):
+                        adapter_pass(acc, s, g, t0 + col, P, col)
+            h, t = divmod(s, PACK)
+            if t == 0:
+                h_rows[group, h] = work.tile([P, PACK, n], BF16, name="h_rows", tag="h_rows", bufs=2)
+            nc.scalar.activation(
+                out=h_rows[group, h][:, t, :], in_=acc[:, 0:n], func=ACT.Relu, bias=a_bias[:, h, t : t + 1]
+            )
+            if step == F_TILES - 1:
+                turned = bank((step + 1) % BANKS)
+                nc.tensor.transpose(turned[:, 0:P], staged32[:], ident[:])
+                nc.scalar.copy(out=by_feature[:], in_=turned[:, 0:P])
+                nc.vector.tensor_tensor(
+                    out=bias_gain[:], in0=by_feature[:, BIAS_ROW : BIAS_ROW + 16],
+                    in1=by_feature[:, GAIN_ROW : GAIN_ROW + 16], op=ALU.mult,
+                )
+            jobs_after("adapter", step)
+
+        def project(u):
+            c, t0, n = UNITS[u]
+            zg[u] = work.tile([P, 4, n], F32, name="zg", tag="zg", bufs=2, align_bytes=64)
+            for i in range(4):
+                acc = next_bank(Z_BANKS)
+                m = 4 * c + i
+                cols = slice(P * m, P * (m + 1))
+                for h in range(F_PASSES):
+                    nc.tensor.matmul_mx(
+                        out=acc[:, 0:n],
+                        lhsT=p_codes[:, h, cols].bitcast(FP8X4),
+                        lhsT_scale=p_plane[:, h, cols],
+                        rhs=h_codes[:, h, t0 : t0 + n].bitcast(FP8X4),
+                        rhs_scale=h_plane[:, h, t0 : t0 + n],
+                        start=(h == 0),
+                        stop=(h == F_PASSES - 1),
+                    )
+                nc.scalar.activation(
+                    out=zg[u][:, i, :], in_=acc[:, 0:n], func=ACT.Identity,
+                    scale=by_feature[:, GAIN_ROW + m : GAIN_ROW + m + 1], bias=bias_gain[:, m : m + 1],
+                )
+                jobs_after("project", u, i)
+
+        def turn_to_frames(u):
+            c, t0, n = UNITS[u]
+            for j0 in range(0, n // P, 2):
+                y[u, j0] = work.tile([P, 2, PASS], F32, name="y", tag="y", bufs=9, align_bytes=64)
+                for j in range(j0, j0 + 2):
+                    acc = next_bank(Y_BANKS)
+                    for i in range(4):
+                        nc.tensor.transpose(acc[:, P * i : P * (i + 1)], zg[u][:, i, P * j : P * (j + 1)], ident[:])
+                    nc.vector.tensor_tensor(
+                        out=y[u, j0][:, j - j0, :], in0=acc[:], in1=embed[c][:, t0 // P + j, :], op=ALU.add
+                    )
+                    jobs_after("added", u, j)
+                frames = slice(t0 + P * j0, t0 + P * (j0 + 2))
+                nc.sync.dma_start(
+                    out=out_0[frames, PASS * c : PASS * (c + 1)].rearrange("(j p) d -> p j d", p=P), in_=y[u, j0][:]
+                )
+                jobs_after("stored", u, j0)
+
+        for c in range(2, CHUNKS):
+            load_embed(c, work.tile([P, T // P, PASS], BF16, name="embed%d" % c, tag="p_raw", bufs=2 * F_PASSES))
+
         project(0)
-        for u in range(last + 2):
-            if u < last:
+        for u in range(LAST + 1):
+            if u < LAST:
                 project(u + 1)
-            wide = u >= 1 and units[u - 1][2] == 512
-            if wide:
-                turn_words(u - 1, 0)
-            fill(2, u, 1, 0)
-            if u <= last:
-                turn_back(u)
-            if u >= 1:
-                turn_words(u - 1, 2 if wide else 0)
-            fill(2, u, 1, 1)
+            jobs_after("before_turn", u)
+            turn_to_frames(u)
+            jobs_after("after_turn", u)
         store_scales(CHUNKS - 1, CHUNKS)

@@ -107,22 +107,22 @@ def tile_speech_adapter_to_language_h2_kernel(
         def bank(n):
             return psum.tile([P, PASS], F32, name="bank%d" % n, tag="bank%d" % n)
 
-        x_codes = [keep.tile([P, K_PASSES, n], U32, name="x_codes%d" % t0, align_bytes=64) for (t0, n) in GROUPS]
-        x_plane = keep.tile([P, K_PASSES, T], U8, name="x_plane", align_bytes=64)
+        x_codes = [keep.tile([P, K_PASSES, n], U32, name="x_codes%d" % t0, align_bytes=256) for (t0, n) in GROUPS]
+        x_plane = keep.tile([P, K_PASSES, T], U8, name="x_plane", align_bytes=256)
         a_codes = [
-            work.tile([P, K_PASSES, 2 * PASS], U8, name="a_codes%d" % h, tag="y", bufs=9, align_bytes=64)
+            work.tile([P, K_PASSES, 2 * PASS], U8, name="a_codes%d" % h, tag="y", bufs=9, align_bytes=256)
             for h in range(F_PASSES)
         ]
-        a_plane = keep.tile([P, F_PASSES, K_PASSES, PASS], U8, name="a_plane", align_bytes=64)
-        a_raw_early = work.tile([P, K_PASSES, 4 * PASS], U8, name="a_raw_early", tag="zg", bufs=2, align_bytes=64)
-        a_raw_late = work.tile([P, K_PASSES, 2 * PASS], U8, name="a_raw_late", tag="y_mixed", bufs=2, align_bytes=64)
-        a_rows_first = work.tile([P, 1, F], U8, name="a_rows_first", tag="y_mixed", bufs=2, align_bytes=64)
-        a_rows_rest = work.tile([P, K_PASSES - 1, F], U8, name="a_rows_rest", tag="zg", bufs=2, align_bytes=64)
-        p_codes = keep.tile([P, F_PASSES, D], U32, name="p_codes", align_bytes=64)
-        p_plane = keep.tile([P, F_PASSES, D], U8, name="p_plane", align_bytes=64)
-        h_codes = keep.tile([P, F_PASSES, T], U32, name="h_codes", align_bytes=64)
-        h_plane = keep.tile([P, F_PASSES, T], U8, name="h_plane", align_bytes=64)
-        y_plane = keep.tile([P, CHUNKS, T], U8, name="y_plane", align_bytes=64)
+        a_plane = keep.tile([P, F_PASSES, K_PASSES, PASS], U8, name="a_plane", align_bytes=256)
+        a_raw_early = work.tile([P, K_PASSES, 4 * PASS], U8, name="a_raw_early", tag="zg", bufs=2, align_bytes=256)
+        a_raw_late = work.tile([P, K_PASSES, 2 * PASS], U8, name="a_raw_late", tag="y_mixed", bufs=2, align_bytes=256)
+        a_rows_first = work.tile([P, 1, F], U8, name="a_rows_first", tag="y_mixed", bufs=2, align_bytes=256)
+        a_rows_rest = work.tile([P, K_PASSES - 1, F], U8, name="a_rows_rest", tag="zg", bufs=2, align_bytes=256)
+        p_codes = keep.tile([P, F_PASSES, D], U32, name="p_codes", align_bytes=256)
+        p_plane = keep.tile([P, F_PASSES, D], U8, name="p_plane", align_bytes=256)
+        h_codes = keep.tile([P, F_PASSES, T], U32, name="h_codes", align_bytes=256)
+        h_plane = keep.tile([P, F_PASSES, T], U8, name="h_plane", align_bytes=256)
+        y_plane = keep.tile([P, CHUNKS, T], U8, name="y_plane", align_bytes=256)
         a_bias = keep.tile([P, F_PASSES, PACK], BF16, name="a_bias")
         staged = keep.tile([P, P], BF16, name="staged")
         staged32 = keep.tile([P, P], F32, name="staged32")
@@ -229,7 +229,7 @@ def tile_speech_adapter_to_language_h2_kernel(
         def mix(engine, key, rows, c0, c1):
             if c0 == 0:
                 mixed[key] = work.tile(
-                    [P, rows.shape[2], PACK], BF16, name="mixed", tag="mixed", bufs=4, align_bytes=64
+                    [P, rows.shape[2], PACK], BF16, name="mixed", tag="mixed", bufs=4, align_bytes=256
                 )
             copy_on[engine](
                 out=mixed[key][:, c0:c1, :].rearrange("p (c i) t -> p c t i", i=4),
@@ -259,7 +259,7 @@ def tile_speech_adapter_to_language_h2_kernel(
         def round_y(engine, u, j0):
             n, nj = UNITS[u][2], frame_tiles(u)
             if j0 == 0:
-                y_pairs[u] = work.tile([P, n // P, PASS], BF16, name="y_pairs", tag="y_pairs", bufs=3, align_bytes=64)
+                y_pairs[u] = work.tile([P, n // P, PASS], BF16, name="y_pairs", tag="y_pairs", bufs=3, align_bytes=256)
             copy_on[engine](
                 out=y_pairs[u][:, j0 : j0 + nj, :].rearrange("p j (v m e) -> p j v m e", v=2, e=2),
                 in_=y[u, j0 - j0 % 2][:, j0 % 2 : j0 % 2 + nj, :].rearrange("p j (m v e) -> p j v m e", v=2, e=2),
@@ -268,7 +268,7 @@ def tile_speech_adapter_to_language_h2_kernel(
         def turn_y(engine, u, j0):
             n, nj = UNITS[u][2], frame_tiles(u)
             if j0 == 0:
-                y_mixed[u] = work.tile([P, n, PACK], BF16, name="y_mixed", tag="y_mixed", bufs=2, align_bytes=64)
+                y_mixed[u] = work.tile([P, n, PACK], BF16, name="y_mixed", tag="y_mixed", bufs=2, align_bytes=256)
             pairs = y_pairs[u][:].bitcast(F32)
             matmuls_done = banks_taken[Z_BANKS] == 4 * len(UNITS)
             acc = next_bank(PAIR_BANKS_AT_END if matmuls_done else PAIR_BANKS)
@@ -292,7 +292,7 @@ def tile_speech_adapter_to_language_h2_kernel(
         def quantize_y(u, j0):
             c, t0, n = UNITS[u]
             m0, m1 = (P * j0, P * (j0 + 1)) if u == LAST else (0, n)
-            y_codes = work.tile([P, m1 - m0], U32, name="y_codes", tag="y_codes", bufs=3, align_bytes=64)
+            y_codes = work.tile([P, m1 - m0], U32, name="y_codes", tag="y_codes", bufs=3, align_bytes=256)
             quantize(y_mixed[u][:, m0:m1, :], y_codes[:], y_plane[:, c, t0 + m0 : t0 + m1])
             nc.sync.dma_start(
                 out=out_1[c].rearrange("p n t -> p (n t)").bitcast(I32)[:, t0 + m0 : t0 + m1],
@@ -362,7 +362,7 @@ def tile_speech_adapter_to_language_h2_kernel(
 
         def project(u):
             c, t0, n = UNITS[u]
-            zg[u] = work.tile([P, 4, n], F32, name="zg", tag="zg", bufs=2, align_bytes=64)
+            zg[u] = work.tile([P, 4, n], F32, name="zg", tag="zg", bufs=2, align_bytes=256)
             for i in range(4):
                 acc = next_bank(Z_BANKS)
                 m = 4 * c + i
@@ -386,7 +386,7 @@ def tile_speech_adapter_to_language_h2_kernel(
         def turn_to_frames(u):
             c, t0, n = UNITS[u]
             for j0 in range(0, n // P, 2):
-                y[u, j0] = work.tile([P, 2, PASS], F32, name="y", tag="y", bufs=9, align_bytes=64)
+                y[u, j0] = work.tile([P, 2, PASS], F32, name="y", tag="y", bufs=9, align_bytes=256)
                 for j in range(j0, j0 + 2):
                     acc = next_bank(Y_BANKS)
                     for i in range(4):

from contextlib import ExitStack

import concourse.mybir as mybir
from concourse.masks import make_identity

T, K, F, D = 768, 2048, 1536, 2048
FLOPS = 2 * T * K * F + 2 * T * F * D

F32 = mybir.dt.float32
BF16 = mybir.dt.bfloat16
I32 = mybir.dt.int32
U32 = mybir.dt.uint32
U8 = mybir.dt.uint8
FP8X4 = mybir.dt.float8_e4m3fn_x4
FP4X4 = mybir.dt.float4_e2m1fn_x4
ACT = mybir.ActivationFunctionType
ALU = mybir.AluOpType

P = 128
PACK = 4
PASS = P * PACK
K_PASSES = K // PASS
F_PASSES = F // PASS
F_TILES = F // P
CHUNKS = D // PASS
GROUPS = ((0, 512), (512, 256))
BANKS = 8
BIAS_ROW, GAIN_ROW = 32, 64

UNITS = [(c, t0, n) for c in range(CHUNKS) for (t0, n) in GROUPS]
LAST = len(UNITS) - 1

Z_BANKS, Y_BANKS, PAIR_BANKS, PAIR_BANKS_AT_END = (1, 3), (4, 4), (0, 1), (0, 4)

VECTOR, SCALAR = "vector", "scalar"

JOBS_AFTER = {
    ("opening",): [("mix_proj", VECTOR, 1, 0, 0, 512)],
    ("adapter", 2): [("mix_proj", VECTOR, 0, 0, 0, 512)],
    ("adapter", 3): [("quantize_proj", 1, 0)],
    ("adapter", 4): [("mix_h", SCALAR, 0, 0), ("quantize_proj", 0, 0)],
    ("adapter", 5): [("mix_proj", VECTOR, 0, 1, 0, 512)],
    ("adapter", 6): [("quantize_h", 0, 0)],
    ("adapter", 8): [("quantize_proj", 0, 1), ("mix_h", VECTOR, 0, 1)],
    ("adapter", 11): [("mix_proj", VECTOR, 0, 2, 0, 512), ("mix_h", SCALAR, 0, 2)],
    ("adapter", 16): [("mix_h", SCALAR, 1, 0), ("quantize_h", 0, 1)],
    ("adapter", 17): [("quantize_proj", 0, 2), ("mix_proj", VECTOR, 1, 2, 0, 512), ("quantize_h", 1, 0)],
    ("adapter", 20): [("quantize_h", 0, 2)],
    ("adapter", 22): [("mix_proj", VECTOR, 1, 1, 0, 512), ("mix_h", SCALAR, 1, 1)],
    ("project", 0, 0): [("quantize_proj", 1, 2), ("quantize_proj", 1, 1)],
    ("project", 0, 1): [("mix_h", VECTOR, 1, 2)],
    ("project", 0, 3): [("quantize_h", 1, 1), ("quantize_h", 1, 2)],
    ("project", 1, 0): [("mix_proj", VECTOR, 2, 1, 0, 512), ("mix_proj", VECTOR, 3, 0, 0, 512)],
    ("project", 1, 1): [("mix_proj", SCALAR, 2, 0, 0, 256)],
    ("project", 1, 2): [("mix_proj", VECTOR, 2, 2, 0, 512)],
    ("before_turn", 0): [("mix_proj", SCALAR, 2, 0, 256, 512)],
    ("after_turn", 0): [("round_y", VECTOR, 0, 0), ("quantize_proj", 2, 1)],
    ("project", 2, 2): [("quantize_proj", 2, 0)],
    ("stored", 1, 0): [("turn_y", SCALAR, 0, 0)],
    ("after_turn", 1): [("quantize_proj", 3, 0)],
    ("project", 3, 0): [("quantize_proj", 2, 2)],
    ("project", 3, 1): [("round_y", SCALAR, 0, 2)],
    ("project", 3, 3): [("round_y", SCALAR, 1, 0), ("mix_proj", VECTOR, 3, 2, 0, 512)],
    ("after_turn", 2): [("turn_y", SCALAR, 0, 2)],
    ("project", 4, 2): [("round_y", VECTOR, 2, 0)],
    ("before_turn", 3): [("round_y", VECTOR, 2, 2)],
    ("stored", 3, 0): [("quantize_y", 0, 0), ("turn_y", SCALAR, 2, 0)],
    ("after_turn", 3): [("mix_proj", VECTOR, 3, 1, 0, 512)],
    ("project", 5, 1): [("quantize_proj", 3, 2)],
    ("project", 5, 3): [("quantize_proj", 3, 1)],
    ("before_turn", 4): [("turn_y", SCALAR, 1, 0), ("quantize_y", 1, 0)],
    ("stored", 4, 2): [("round_y", VECTOR, 3, 0), ("turn_y", SCALAR, 2, 2)],
    ("project", 6, 0): [("round_y", SCALAR, 4, 0)],
    ("project", 6, 1): [("quantize_y", 2, 0)],
    ("after_turn", 5): [("turn_y", VECTOR, 3, 0), ("round_y", VECTOR, 5, 0)],
    ("project", 7, 0): [("quantize_y", 3, 0)],
    ("project", 7, 2): [("round_y", SCALAR, 4, 2)],
    ("stored", 6, 0): [("turn_y", SCALAR, 5, 0)],
    ("after_turn", 6): [("turn_y", SCALAR, 4, 0), ("turn_y", VECTOR, 4, 2), ("quantize_y", 4, 0)],
    ("before_turn", 7): [("round_y", SCALAR, 6, 0), ("quantize_y", 5, 0)],
    ("added", 7, 0): [("round_y", SCALAR, 6, 2)],
    ("added", 7, 1): [("turn_y", SCALAR, 6, 0), ("round_y", SCALAR, 7, 0)],
    ("after_turn", 7): [
        ("turn_y", VECTOR, 6, 2),
        ("round_y", VECTOR, 7, 1),
        ("turn_y", SCALAR, 7, 0),
        ("quantize_y", 6, 0),
        ("turn_y", SCALAR, 7, 1),
        ("quantize_y", 7, 1),
        ("quantize_y", 7, 0),
    ],
}


def tile_speech_adapter_to_language_h2_kernel(
    tc, x_words, x_scales, adapter_words, adapter_scales, adapter_bias, proj, proj_bias,
    feature_gain, time_embed, out_0, out_1, out_2,
):
    nc = tc.nc
    copy_on = {VECTOR: nc.vector.tensor_copy, SCALAR: nc.scalar.copy}
    with ExitStack() as ctx:
        keep = ctx.enter_context(tc.tile_pool(name="keep", bufs=1))
        work = ctx.enter_context(tc.tile_pool(name="work", bufs=2))
        psum = ctx.enter_context(tc.psum_pool(name="psum", bufs=1))
        ctx.enter_context(tc.manual_schedule())

        def bank(n):
            return psum.tile([P, PASS], F32, name="bank%d" % n, tag="bank%d" % n)

        x_codes = [keep.tile([P, K_PASSES, n], U32, name="x_codes%d" % t0, align_bytes=256) for (t0, n) in GROUPS]
        x_plane = keep.tile([P, K_PASSES, T], U8, name="x_plane", align_bytes=256)
        a_codes = [
            work.tile([P, K_PASSES, 2 * PASS], U8, name="a_codes%d" % h, tag="y", bufs=9, align_bytes=256)
            for h in range(F_PASSES)
        ]
        a_plane = keep.tile([P, F_PASSES, K_PASSES, PASS], U8, name="a_plane", align_bytes=256)
        a_raw_early = work.tile([P, K_PASSES, 4 * PASS], U8, name="a_raw_early", tag="zg", bufs=2, align_bytes=256)
        a_raw_late = work.tile([P, K_PASSES, 2 * PASS], U8, name="a_raw_late", tag="y_mixed", bufs=2, align_bytes=256)
        a_rows_first = work.tile([P, 1, F], U8, name="a_rows_first", tag="y_mixed", bufs=2, align_bytes=256)
        a_rows_rest = work.tile([P, K_PASSES - 1, F], U8, name="a_rows_rest", tag="zg", bufs=2, align_bytes=256)
        p_codes = keep.tile([P, F_PASSES, D], U32, name="p_codes", align_bytes=256)
        p_plane = keep.tile([P, F_PASSES, D], U8, name="p_plane", align_bytes=256)
        h_codes = keep.tile([P, F_PASSES, T], U32, name="h_codes", align_bytes=256)
        h_plane = keep.tile([P, F_PASSES, T], U8, name="h_plane", align_bytes=256)
        y_plane = keep.tile([P, CHUNKS, T], U8, name="y_plane", align_bytes=256)
        a_bias = keep.tile([P, F_PASSES, PACK], BF16, name="a_bias")
        staged = keep.tile([P, P], BF16, name="staged")
        staged32 = keep.tile([P, P], F32, name="staged32")
        ident = keep.tile([P, P], F32, name="ident")
        by_feature = keep.tile([P, P], F32, name="by_feature")
        bias_gain = keep.tile([P, D // P], F32, name="bias_gain")

        x_words32 = x_words.rearrange("g p n t -> p g (n t)").bitcast(I32)
        a_words32 = adapter_words.rearrange("g p n -> p g n").bitcast(I32)
        a_scales32 = adapter_scales.rearrange("g q n -> q g n").bitcast(I32)
        x_scales32 = x_scales.rearrange("g q n -> q g n").bitcast(I32)
        proj_rows = proj.rearrange("(h p t) d -> h p t d", h=F_PASSES, t=PACK)
        p_raw = {}
        embed = {}

        def load_words(g):
            nc.sync.dma_start(out=a_raw_early[:, g, :].bitcast(I32), in_=a_words32[:, g, 0:PASS])
            nc.sync.dma_start(out=x_codes[0][:, g, :].bitcast(I32), in_=x_words32[:, g, 0:PASS])

        def load_scale_rows(plane, rows):
            for r in range(4):
                nc.sync.dma_start(out=plane[:].bitcast(I32)[r:P:32, :, :], in_=rows[r:16:4, :, :])

        def load_proj(half, h):
            p_raw[half, h] = work.tile(
                [P, PACK, 2 * PASS], BF16, name="p_raw%d%d" % (half, h), tag="p_raw", bufs=2 * F_PASSES
            )
            cols = slice(2 * PASS * half, 2 * PASS * (half + 1))
            nc.sync.dma_start(out=p_raw[half, h][:], in_=proj_rows[h][:, :, cols])

        def load_embed(c, tile):
            embed[c] = tile
            cols = slice(PASS * c, PASS * (c + 1))
            nc.sync.dma_start(out=tile[:], in_=time_embed[:, cols].rearrange("(j p) d -> p j d", p=P))

        nc.vector.memset(a_rows_first[:].bitcast(I32), 0)
        nc.vector.memset(x_plane[:].bitcast(I32), 0)
        nc.vector.memset(a_rows_rest[:].bitcast(I32), 0)
        nc.vector.memset(staged[:], 0.0)
        make_identity(nc, ident[:])
        load_words(0)
        load_scale_rows(a_rows_first, a_scales32[:, 0:1, :])
        load_scale_rows(x_plane, x_scales32)
        load_scale_rows(a_rows_rest, a_scales32[:, 1:K_PASSES, :])
        load_words(1)
        nc.sync.dma_start(out=a_bias[:], in_=adapter_bias.rearrange("(h p t) -> p h t", p=P, t=PACK))
        nc.sync.dma_start(out=staged[BIAS_ROW : BIAS_ROW + 16, :], in_=proj_bias.rearrange("(m p) -> m p", p=P))
        nc.sync.dma_start(out=staged[GAIN_ROW : GAIN_ROW + 16, :], in_=feature_gain.rearrange("(m p) -> m p", p=P))
        load_words(2)
        load_words(3)
        nc.sync.dma_start(out=a_raw_late[:].bitcast(I32), in_=a_words32[:, :, PASS : F // 2])
        load_proj(0, 0)
        load_proj(0, 1)
        nc.sync.dma_start(out=x_codes[1][:].bitcast(I32), in_=x_words32[:, :, PASS:T])
        load_proj(0, 2)
        load_proj(1, 0)
        load_embed(0, keep.tile([P, T // P, PASS], BF16, name="embed0"))
        load_proj(1, 1)
        load_embed(1, keep.tile([P, T // P, PASS], BF16, name="embed1"))
        load_proj(1, 2)

        def reorder_words(h, g):
            raw = a_raw_early[:, g, 2 * PASS * h : 2 * PASS * (h + 1)] if h < 2 else a_raw_late[:, g, :]
            nc.vector.tensor_copy(
                out=a_codes[h][:, g, :].rearrange("p (t m e) -> p t m e", t=PACK, e=2),
                in_=raw.rearrange("p (m t e) -> p t m e", t=PACK, e=2),
            )

        def reorder_scales(h, g):
            raw = (a_rows_first[:, 0, :] if g == 0 else a_rows_rest[:, g - 1, :])[:, PASS * h : PASS * (h + 1)]
            nc.vector.tensor_copy(
                out=a_plane[:, h, g, :].rearrange("p (t m) -> p t m", t=PACK),
                in_=raw.rearrange("p (m t) -> p t m", t=PACK),
            )

        for h in range(2):
            reorder_words(h, 0)
        for h in range(F_PASSES):
            reorder_scales(h, 0)
        for h in range(2):
            reorder_scales(h, 1)
        for h in range(2):
            reorder_words(h, 1)
        for g in (2, 3):
            for h in range(2):
                reorder_scales(h, g)
            reorder_words(0, g)
        for g in (2, 3):
            reorder_words(1, g)
        for g in range(1, K_PASSES):
            reorder_scales(2, g)
        for g in range(K_PASSES):
            reorder_words(2, g)

        h_rows, mixed, zg, y, y_pairs, y_mixed = {}, {}, {}, {}, {}, {}
        banks_taken = {}

        def next_bank(banks):
            first, count = banks
            taken = banks_taken.get(banks, 0)
            banks_taken[banks] = taken + 1
            return bank(first + taken % count)

        def mix(engine, key, rows, c0, c1):
            if c0 == 0:
                mixed[key] = work.tile(
                    [P, rows.shape[2], PACK], BF16, name="mixed", tag="mixed", bufs=4, align_bytes=256
                )
            copy_on[engine](
                out=mixed[key][:, c0:c1, :].rearrange("p (c i) t -> p c t i", i=4),
                in_=rows[:, :, c0:c1].rearrange("p t (c i) -> p c t i", i=4),
            )

        def quantize(source, codes, plane):
            nc.vector.quantize_mx(out=codes.bitcast(FP8X4), scales=plane, in_=source.rearrange("p n t -> p (n t)"))

        def mix_proj(engine, c, h, c0, c1):
            mix(engine, ("proj", c, h), p_raw[c // 2, h][:, :, PASS * (c % 2) : PASS * (c % 2 + 1)], c0, c1)

        def quantize_proj(c, h):
            cols = slice(PASS * c, PASS * (c + 1))
            quantize(mixed["proj", c, h][:], p_codes[:, h, cols], p_plane[:, h, cols])

        def mix_h(engine, group, h):
            mix(engine, ("h", group, h), h_rows[group, h], 0, GROUPS[group][1])

        def quantize_h(group, h):
            t0, n = GROUPS[group]
            quantize(mixed["h", group, h][:], h_codes[:, h, t0 : t0 + n], h_plane[:, h, t0 : t0 + n])

        def frame_tiles(u):
            return 1 if u == LAST else 2

        def round_y(engine, u, j0):
            n, nj = UNITS[u][2], frame_tiles(u)
            if j0 == 0:
                y_pairs[u] = work.tile([P, n // P, PASS], BF16, name="y_pairs", tag="y_pairs", bufs=3, align_bytes=256)
            copy_on[engine](
                out=y_pairs[u][:, j0 : j0 + nj, :].rearrange("p j (v m e) -> p j v m e", v=2, e=2),
                in_=y[u, j0 - j0 % 2][:, j0 % 2 : j0 % 2 + nj, :].rearrange("p j (m v e) -> p j v m e", v=2, e=2),
            )

        def turn_y(engine, u, j0):
            n, nj = UNITS[u][2], frame_tiles(u)
            if j0 == 0:
                y_mixed[u] = work.tile([P, n, PACK], BF16, name="y_mixed", tag="y_mixed", bufs=2, align_bytes=256)
            pairs = y_pairs[u][:].bitcast(F32)
            matmuls_done = banks_taken[Z_BANKS] == 4 * len(UNITS)
            acc = next_bank(PAIR_BANKS_AT_END if matmuls_done else PAIR_BANKS)
            for jj in range(nj):
                for v in range(2):
                    col = P * (2 * jj + v)
                    nc.tensor.transpose(acc[:, col : col + P], pairs[:, j0 + jj, P * v : P * (v + 1)], ident[:])
            copy_on[engine](
                out=y_mixed[u][:, P * j0 : P * (j0 + nj), :].bitcast(F32).rearrange("p (j m) v -> p j m v", j=nj),
                in_=acc[:, 0 : 2 * P * nj].rearrange("p (j v m) -> p j m v", j=nj, v=2),
            )

        def store_scales(c0, c1):
            for r in range(4):
                queue = nc.scalar if c1 == CHUNKS and r % 2 else nc.sync
                queue.dma_start(
                    out=out_2[c0:c1, r:16:4, :].rearrange("g q n -> q g n").bitcast(I32),
                    in_=y_plane[r:P:32, c0:c1, :].bitcast(I32),
                )

        def quantize_y(u, j0):
            c, t0, n = UNITS[u]
            m0, m1 = (P * j0, P * (j0 + 1)) if u == LAST else (0, n)
            y_codes = work.tile([P, m1 - m0], U32, name="y_codes", tag="y_codes", bufs=3, align_bytes=256)
            quantize(y_mixed[u][:, m0:m1, :], y_codes[:], y_plane[:, c, t0 + m0 : t0 + m1])
            nc.sync.dma_start(
                out=out_1[c].rearrange("p n t -> p (n t)").bitcast(I32)[:, t0 + m0 : t0 + m1],
                in_=y_codes[:].bitcast(I32),
            )
            if u == LAST - len(GROUPS):
                store_scales(0, CHUNKS - 1)

        jobs = {
            "mix_proj": mix_proj, "quantize_proj": quantize_proj, "mix_h": mix_h, "quantize_h": quantize_h,
            "round_y": round_y, "turn_y": turn_y, "quantize_y": quantize_y,
        }

        def jobs_after(*step):
            for job in JOBS_AFTER.get(step, ()):
                jobs[job[0]](*job[1:])

        def adapter_pass(acc, s, g, t0, n, col):
            h, t = divmod(s, PACK)
            nc.tensor.matmul_mx(
                out=acc[:, col : col + n],
                lhsT=a_codes[h][:, g, 2 * P * t : 2 * P * (t + 1)].bitcast(FP4X4),
                lhsT_scale=a_plane[:, h, g, P * t : P * (t + 1)],
                rhs=x_codes[t0 // PASS][:, g, t0 % PASS : t0 % PASS + n].bitcast(FP8X4),
                rhs_scale=x_plane[:, g, t0 : t0 + n],
                start=(g == 0),
                stop=(g == K_PASSES - 1),
            )

        opened = [bank(s) for s in range(BANKS)]
        for g in range(2):
            for s in range(BANKS):
                adapter_pass(opened[s], s, g, 0, PASS, 0)
        nc.scalar.activation(out=staged32[:], in_=staged[:], func=ACT.Identity)
        jobs_after("opening")
        for step in range(2 * F_TILES):
            group, s = divmod(step, F_TILES)
            t0, n = GROUPS[group]
            if step < BANKS:
                acc = opened[step]
                for g in range(2, K_PASSES):
                    adapter_pass(acc, s, g, t0, n, 0)
            elif group == 0:
                acc = bank(step % BANKS)
                for g in range(K_PASSES):
                    adapter_pass(acc, s, g, t0, n, 0)
            else:
                acc = bank((step + 1) % BANKS)
                for col in range(0, n, P):
                    for g in range(K_PASSES):
                        adapter_pass(acc, s, g, t0 + col, P, col)
            h, t = divmod(s, PACK)
            if t == 0:
                h_rows[group, h] = work.tile([P, PACK, n], BF16, name="h_rows", tag="h_rows", bufs=2)
            nc.scalar.activation(
                out=h_rows[group, h][:, t, :], in_=acc[:, 0:n], func=ACT.Relu, bias=a_bias[:, h, t : t + 1]
            )
            if step == F_TILES - 1:
                turned = bank((step + 1) % BANKS)
                nc.tensor.transpose(turned[:, 0:P], staged32[:], ident[:])
                nc.scalar.copy(out=by_feature[:], in_=turned[:, 0:P])
                nc.vector.tensor_tensor(
                    out=bias_gain[:], in0=by_feature[:, BIAS_ROW : BIAS_ROW + 16],
                    in1=by_feature[:, GAIN_ROW : GAIN_ROW + 16], op=ALU.mult,
                )
            jobs_after("adapter", step)

        def project(u):
            c, t0, n = UNITS[u]
            zg[u] = work.tile([P, 4, n], F32, name="zg", tag="zg", bufs=2, align_bytes=256)
            for i in range(4):
                acc = next_bank(Z_BANKS)
                m = 4 * c + i
                cols = slice(P * m, P * (m + 1))
                for h in range(F_PASSES):
                    nc.tensor.matmul_mx(
                        out=acc[:, 0:n],
                        lhsT=p_codes[:, h, cols].bitcast(FP8X4),
                        lhsT_scale=p_plane[:, h, cols],
                        rhs=h_codes[:, h, t0 : t0 + n].bitcast(FP8X4),
                        rhs_scale=h_plane[:, h, t0 : t0 + n],
                        start=(h == 0),
                        stop=(h == F_PASSES - 1),
                    )
                nc.scalar.activation(
                    out=zg[u][:, i, :], in_=acc[:, 0:n], func=ACT.Identity,
                    scale=by_feature[:, GAIN_ROW + m : GAIN_ROW + m + 1], bias=bias_gain[:, m : m + 1],
                )
                jobs_after("project", u, i)

        def turn_to_frames(u):
            c, t0, n = UNITS[u]
            for j0 in range(0, n // P, 2):
                y[u, j0] = work.tile([P, 2, PASS], F32, name="y", tag="y", bufs=9, align_bytes=256)
                for j in range(j0, j0 + 2):
                    acc = next_bank(Y_BANKS)
                    for i in range(4):
                        nc.tensor.transpose(acc[:, P * i : P * (i + 1)], zg[u][:, i, P * j : P * (j + 1)], ident[:])
                    nc.vector.tensor_tensor(
                        out=y[u, j0][:, j - j0, :], in0=acc[:], in1=embed[c][:, t0 // P + j, :], op=ALU.add
                    )
                    jobs_after("added", u, j)
                frames = slice(t0 + P * j0, t0 + P * (j0 + 2))
                nc.sync.dma_start(
                    out=out_0[frames, PASS * c : PASS * (c + 1)].rearrange("(j p) d -> p j d", p=P), in_=y[u, j0][:]
                )
                jobs_after("stored", u, j0)

        for c in range(2, CHUNKS):
            load_embed(c, work.tile([P, T // P, PASS], BF16, name="embed%d" % c, tag="p_raw", bufs=2 * F_PASSES))

        project(0)
        for u in range(LAST + 1):
            if u < LAST:
                project(u + 1)
            jobs_after("before_turn", u)
            turn_to_frames(u)
            jobs_after("after_turn", u)
        store_scales(CHUNKS - 1, CHUNKS)
